import numpy as np
import ml_dtypes


def mxq(x, axis, fmt="e4m3"):
    dtype, down = {"e4m3": (ml_dtypes.float8_e4m3fn, 7), "e5m2": (ml_dtypes.float8_e5m2, 14)}[fmt]
    v = np.moveaxis(np.asarray(x, np.float32).astype(ml_dtypes.bfloat16).astype(np.float64), axis, -1)
    blocks = v.reshape(v.shape[:-1] + (-1, 32))
    amax = np.abs(blocks).max(-1, keepdims=True)
    byte = np.maximum(np.where(amax > 0, np.frexp(amax)[1] - 1 + 127, 0) - down, 1)
    scale = np.exp2(byte - 127.0)
    codes = (blocks / scale).astype(np.float32).astype(dtype).astype(np.float64)
    return np.moveaxis((codes * scale).reshape(v.shape), -1, axis)


WIDE = False


def mx_kscale(k):
    if not WIDE:
        return np.ones(k)
    levels = np.array([10, -10, 5, -5, 0])
    if k % 512:
        return np.exp2(np.random.permutation(np.resize(levels, k // 32))).repeat(32)
    a = np.empty((k // 512, 16))
    for p in range(k // 512):
        a[p, :8] = np.random.permutation(np.resize(levels, 8))
        for g in range(8):
            far = levels[np.abs(levels - a[p, g]) >= 10]
            a[p, g + 8] = far[np.random.randint(len(far))]
    return np.exp2(a.ravel()).repeat(32)


def f64(x):
    return np.asarray(x).astype(np.float64)


def striped(idx):
    return np.tile(idx.reshape(-1, 16).T, (8, 1)).astype(np.uint16)


def unstriped(offs):
    return offs[:16].T.reshape(-1).astype(np.int64)


def striped8(idx):
    return np.concatenate([x.reshape(-1, 16).T for x in idx]).astype(np.uint16)


def runs(offs, k):
    lists = np.stack([offs[16 * r : 16 * r + 16].T.reshape(-1) for r in range(8)]).astype(np.int64)
    return lists[np.arange(k) % 512 // 64]


def pack_weight(w):
    k, n = w.shape
    w = f64(np.asarray(w, np.float32).astype(ml_dtypes.bfloat16)).reshape(k // 32, 32, n)
    amax = np.abs(w).max(1)
    byte = np.clip(np.where(amax > 0, np.frexp(amax)[1] - 1 + 127 - 7, 1), 1, 254)
    scaled = (w * np.exp2(127.0 - byte)[:, None, :]).reshape(k, n).astype(np.float32)
    words = np.ascontiguousarray(scaled.reshape(k // 512, 128, 4, n).transpose(0, 1, 3, 2)).astype(ml_dtypes.float8_e4m3fn).view(np.uint8)
    return words, np.ascontiguousarray(byte.astype(np.uint8).reshape(k // 512, 16, n))


def unpack_weight(words, scales):
    g, p, n, _ = words.shape
    vals = np.ascontiguousarray(words).view(ml_dtypes.float8_e4m3fn).astype(np.float64) * np.repeat(np.exp2(scales.astype(np.float64) - 127.0), 8, axis=1)[..., None]
    return vals.transpose(0, 1, 3, 2).reshape(g * 512, n)


K, T, S, V, N, H = 512, 2048, 512, 256, 512, 512


def setup_inputs():
    n = np.random.standard_normal
    s = mx_kscale(K)[:, None]
    u = mx_kscale(H)
    packed_xT = pack_weight(n((K, T)) * s)
    perm = np.stack([np.random.permutation(S) for _ in range(8)])
    return {
        "x_words": packed_xT[0],
        "x_scales": packed_xT[1],
        "w1": (n((K, H)) / np.sqrt(K) / s * u).astype(np.float32),
        "w2": (n((H, N)) / np.sqrt(H) / u[:, None]).astype(np.float32),
        "offs": striped(np.random.permutation(T)[:S]),
        "la": striped8(perm[:, :V]),
        "lb": striped8(perm[:, V:]),
    }


def reference(x_words, x_scales, w1, w2, offs, la, lb):
    xq = unpack_weight(x_words, x_scales)[:, unstriped(offs)]
    y = mxq(f64(w1), 0, "e4m3").T @ xq
    a = y[np.arange(H)[:, None], runs(la, H)]
    b = y[np.arange(H)[:, None], runs(lb, H)]
    df = 0.75 * (a - b)
    sm = 0.75 * (a + b)
    p = np.zeros((H, S))
    p[np.arange(H)[:, None], runs(la, H)] = sm
    z = p.copy()
    z[np.arange(H)[:, None], runs(lb, H)] = df
    return mxq(f64(w2), 0, "e4m3").T @ mxq(z, 0, "e4m3")

@@ -1,0 +1,173 @@
+from contextlib import ExitStack
+
+import concourse.mybir as mybir
+
+K, T, S, V, N, H = 512, 2048, 512, 256, 512, 512
+FLOPS = 2 * K * H * S + 2 * H * N * S
+
+F32 = mybir.dt.float32
+BF16 = mybir.dt.bfloat16
+I32 = mybir.dt.int32
+U32 = mybir.dt.uint32
+U16 = mybir.dt.uint16
+U8 = mybir.dt.uint8
+FP8X4 = mybir.dt.float8_e4m3fn_x4
+COPY = mybir.ActivationFunctionType.Copy
+ADD = mybir.AluOpType.add
+
+P = 128
+PACK = 4
+HALF = S // 2
+W1_SCALAR_M = 40
+
+
+def tile_picked_haarinp_none_p_kernel(tc, x_words, x_scales, w1, w2, offs, la, lb, out):
+    nc = tc.nc
+    with ExitStack() as ctx:
+        lists = ctx.enter_context(tc.tile_pool(name="lists", bufs=1))
+        keep = ctx.enter_context(tc.tile_pool(name="keep", bufs=1))
+        psum = ctx.enter_context(tc.psum_pool(name="psum", bufs=8))
+
+        offs_sb = lists.tile([P, S // 16], U16, name="offs_sb")
+        la_sb = lists.tile([P, V // 16], U16, name="la_sb")
+        lb_sb = lists.tile([P, V // 16], U16, name="lb_sb")
+
+        w1_raw = keep.tile([P, PACK, H], F32, name="w1_raw")
+        x_table = keep.tile([P, T], I32, name="x_table")
+        s_table = keep.tile([P, T], U8, name="s_table")
+        w2_raw = keep.tile([P, PACK, N], F32, name="w2_raw")
+
+        nc.vector.memset(s_table[:].bitcast(I32), 0)
+        nc.sync.dma_start(out=w1_raw[:], in_=w1.rearrange("(p j) c -> p j c", j=PACK))
+        nc.sync.dma_start(offs_sb[:], offs)
+        for q in range(4):
+            nc.scalar.dma_start(
+                out=s_table[32 * q : 32 * q + 4, :].bitcast(I32),
+                in_=x_scales[0, 4 * q : 4 * q + 4, :].bitcast(I32),
+            )
+        nc.sync.dma_start(out=x_table[:], in_=x_words[0].rearrange("p n t -> p (n t)").bitcast(I32))
+        nc.sync.dma_start(la_sb[:], la)
+        nc.sync.dma_start(lb_sb[:], lb)
+        nc.sync.dma_start(out=w2_raw[:], in_=w2.rearrange("(p j) c -> p j c", j=PACK))
+
+        x_sc = keep.tile([P, S], U8, name="x_sc", align_bytes=64)
+        nc.vector.tensor_copy(out=x_sc[:], in_=s_table[:].indirect(offs_sb[:]))
+
+        w1_grouped = keep.tile([P, PACK * H], BF16, name="w1_grouped", align_bytes=64)
+        dst = w1_grouped[:].rearrange("p (t m j) -> p m j t", t=PACK, j=PACK)
+        src = w1_raw[:].rearrange("p j (m t) -> p m j t", t=PACK)
+        nc.scalar.activation(out=dst[:, :W1_SCALAR_M], in_=src[:, :W1_SCALAR_M], func=COPY)
+        nc.vector.tensor_copy(out=dst[:, W1_SCALAR_M:], in_=src[:, W1_SCALAR_M:])
+        w1_codes = keep.tile([P, H], U32, name="w1_codes", align_bytes=64)
+        w1_sc = keep.tile([P, H], U8, name="w1_sc", align_bytes=64)
+        nc.vector.quantize_mx(out=w1_codes[:].bitcast(FP8X4), scales=w1_sc[:], in_=w1_grouped[:])
+
+        x_codes = keep.tile([P, S], U32, name="x_codes", align_bytes=64)
+        for h in range(2):
+            nc.vector.tensor_copy(
+                out=x_codes[:, h * HALF : (h + 1) * HALF],
+                in_=x_table[:].bitcast(U32).indirect(offs_sb[:, h * HALF // 16 : (h + 1) * HALF // 16]),
+            )
+
+        y = [keep.tile([P, S], F32, name="y%d" % t) for t in range(PACK)]
+
+        def first_product(t, c0, c1):
+            acc = psum.tile([P, c1 - c0], F32, name="acc", tag="bank")
+            nc.tensor.matmul_mx(
+                out=acc[:],
+                lhsT=w1_codes[:, t * P : (t + 1) * P].bitcast(FP8X4),
+                lhsT_scale=w1_sc[:, t * P : (t + 1) * P],
+                rhs=x_codes[:, c0:c1].bitcast(FP8X4),
+                rhs_scale=x_sc[:, c0:c1],
+                start=True,
+                stop=True,
+            )
+            nc.scalar.activation(out=y[t][:, c0:c1], in_=acc[:], func=COPY, scale=0.75)
+
+        first_product(0, 0, HALF)
+        first_product(0, HALF, S)
+        for t in range(1, PACK):
+            first_product(t, 0, S)
+
+        a = [keep.tile([P, V], F32, name="a%d" % t) for t in range(PACK)]
+        b = [keep.tile([P, V], F32, name="b%d" % t) for t in range(PACK)]
+        nb = [keep.tile([P, V], F32, name="nb%d" % t) for t in range(PACK)]
+        z = [keep.tile([P, S], F32, name="z%d" % t) for t in range(PACK - 1)]
+        z_grouped = keep.tile([P, S, PACK], BF16, name="z_grouped", align_bytes=64)
+
+        def fetch(t):
+            nc.vector.tensor_copy(out=b[t][:], in_=y[t][:].indirect(lb_sb[:]))
+            nc.vector.tensor_copy(out=a[t][:], in_=y[t][:].indirect(la_sb[:]))
+            nc.scalar.activation(out=nb[t][:], in_=b[t][:], func=COPY, scale=-1.0)
+
+        def put_sum(t):
+            nc.vector.tensor_tensor(z[t][:].indirect(la_sb[:]), a[t][:], b[t][:], ADD)
+
+        def put_diff(t):
+            nc.vector.tensor_tensor(z[t][:].indirect(lb_sb[:]), a[t][:], nb[t][:], ADD)
+
+        def round_scalar(t, c0, c1):
+            nc.scalar.copy(out=z_grouped[:, c0:c1, t], in_=z[t][:, c0:c1])
+
+        fetch(0)
+        fetch(1)
+        put_sum(0)
+        put_sum(1)
+        put_diff(0)
+        fetch(2)
+
+        w2_grouped = keep.tile([P, N * PACK], BF16, name="w2_grouped", tag="shared", align_bytes=64)
+        dst2 = w2_grouped[:].rearrange("p (c i j) -> p c j i", i=4, j=PACK)
+        src2 = w2_raw[:].rearrange("p j (c i) -> p c j i", i=4)
+        for piece in range(4):
+            nc.scalar.copy(out=dst2[:, piece * 32 : (piece + 1) * 32], in_=src2[:, piece * 32 : (piece + 1) * 32])
+        w2_codes = keep.tile([P, N], U32, name="w2_codes", align_bytes=64)
+        w2_sc = keep.tile([P, N], U8, name="w2_sc", align_bytes=64)
+
+        put_sum(2)
+        put_diff(1)
+        fetch(3)
+        round_scalar(0, 0, S)
+        round_scalar(1, 0, S)
+        nc.vector.quantize_mx(out=w2_codes[:].bitcast(FP8X4), scales=w2_sc[:], in_=w2_grouped[:])
+        z.append(keep.tile([P, S], F32, name="z3", tag="shared", align_bytes=64))
+        put_sum(3)
+        put_diff(2)
+        put_diff(3)
+        round_scalar(2, 0, S)
+
+        z_codes = keep.tile([P, S], U32, name="z_codes", align_bytes=64)
+        z_sc = keep.tile([P, S], U8, name="z_sc", align_bytes=64)
+        out_blocks = out.rearrange("(u p) c -> p u c", p=P)
+        chunks = [(0, 128), (128, 256), (256, 512)]
+        for c0, c1 in chunks:
+            round_scalar(3, c0, c1)
+            nc.vector.quantize_mx(
+                out=z_codes[:, c0:c1].bitcast(FP8X4),
+                scales=z_sc[:, c0:c1],
+                in_=z_grouped[:, c0:c1, :].rearrange("p c t -> p (c t)"),
+            )
+        bank = 0
+        for c0, c1 in chunks:
+            width = c1 - c0
+            per_bank = HALF // width
+            for u0 in range(0, N // P, per_bank):
+                acc = psum.tile([P, per_bank, width], F32, name="acc", tag="bank")
+                for du in range(per_bank):
+                    rows = slice((u0 + du) * P, (u0 + du + 1) * P)
+                    nc.tensor.matmul_mx(
+                        out=acc[:, du, :],
+                        lhsT=w2_codes[:, rows].bitcast(FP8X4),
+                        lhsT_scale=w2_sc[:, rows],
+                        rhs=z_codes[:, c0:c1].bitcast(FP8X4),
+                        rhs_scale=z_sc[:, c0:c1],
+                        start=True,
+                        stop=True,
+                    )
+                res = keep.tile([P, per_bank, width], F32, name="res%d" % bank)
+                if bank >= 3 and bank % 2 == 1:
+                    nc.scalar.copy(out=res[:], in_=acc[:])
+                else:
+                    nc.vector.tensor_copy(out=res[:], in_=acc[:])
+                nc.sync.dma_start(out=out_blocks[:, u0 : u0 + per_bank, c0:c1], in_=res[:])
+                bank = bank + 1

@@ -18,7 +18,7 @@ ADD = mybir.AluOpType.add
 P = 128
 PACK = 4
 HALF = S // 2
-W1_SCALAR_M = 40
+W1_SCALAR_M = 72
 
 
 def tile_picked_haarinp_none_p_kernel(tc, x_words, x_scales, w1, w2, offs, la, lb, out):
@@ -34,31 +34,31 @@ def tile_picked_haarinp_none_p_kernel(tc, x_words, x_scales, w1, w2, offs, la, l
 
         w1_raw = keep.tile([P, PACK, H], F32, name="w1_raw")
         x_table = keep.tile([P, T], I32, name="x_table")
-        s_table = keep.tile([P, T], U8, name="s_table")
+        s_table = keep.tile([P, T], U8, name="s_table", tag="scale_rows", align_bytes=64)
         w2_raw = keep.tile([P, PACK, N], F32, name="w2_raw")
 
         nc.vector.memset(s_table[:].bitcast(I32), 0)
-        nc.sync.dma_start(out=w1_raw[:], in_=w1.rearrange("(p j) c -> p j c", j=PACK))
         nc.sync.dma_start(offs_sb[:], offs)
+        nc.sync.dma_start(out=w1_raw[:], in_=w1.rearrange("(p j) c -> p j c", j=PACK))
+        nc.sync.dma_start(la_sb[:], la)
+        nc.sync.dma_start(lb_sb[:], lb)
         for q in range(4):
-            nc.scalar.dma_start(
+            nc.sync.dma_start(
                 out=s_table[32 * q : 32 * q + 4, :].bitcast(I32),
                 in_=x_scales[0, 4 * q : 4 * q + 4, :].bitcast(I32),
             )
         nc.sync.dma_start(out=x_table[:], in_=x_words[0].rearrange("p n t -> p (n t)").bitcast(I32))
-        nc.sync.dma_start(la_sb[:], la)
-        nc.sync.dma_start(lb_sb[:], lb)
         nc.sync.dma_start(out=w2_raw[:], in_=w2.rearrange("(p j) c -> p j c", j=PACK))
-
-        x_sc = keep.tile([P, S], U8, name="x_sc", align_bytes=64)
-        nc.vector.tensor_copy(out=x_sc[:], in_=s_table[:].indirect(offs_sb[:]))
 
         w1_grouped = keep.tile([P, PACK * H], BF16, name="w1_grouped", align_bytes=64)
         dst = w1_grouped[:].rearrange("p (t m j) -> p m j t", t=PACK, j=PACK)
         src = w1_raw[:].rearrange("p j (m t) -> p m j t", t=PACK)
         nc.scalar.activation(out=dst[:, :W1_SCALAR_M], in_=src[:, :W1_SCALAR_M], func=COPY)
         nc.vector.tensor_copy(out=dst[:, W1_SCALAR_M:], in_=src[:, W1_SCALAR_M:])
-        w1_codes = keep.tile([P, H], U32, name="w1_codes", align_bytes=64)
+        x_sc = keep.tile([P, S], U8, name="x_sc", align_bytes=64)
+        nc.vector.tensor_copy(out=x_sc[:], in_=s_table[:].indirect(offs_sb[:]))
+
+        w1_codes = keep.tile([P, H], U32, name="w1_codes", tag="scale_rows", align_bytes=64)
         w1_sc = keep.tile([P, H], U8, name="w1_sc", align_bytes=64)
         nc.vector.quantize_mx(out=w1_codes[:].bitcast(FP8X4), scales=w1_sc[:], in_=w1_grouped[:])
 
@@ -89,15 +89,18 @@ def tile_picked_haarinp_none_p_kernel(tc, x_words, x_scales, w1, w2, offs, la, l
         for t in range(1, PACK):
             first_product(t, 0, S)
 
-        a = [keep.tile([P, V], F32, name="a%d" % t) for t in range(PACK)]
-        b = [keep.tile([P, V], F32, name="b%d" % t) for t in range(PACK)]
-        nb = [keep.tile([P, V], F32, name="nb%d" % t) for t in range(PACK)]
-        z = [keep.tile([P, S], F32, name="z%d" % t) for t in range(PACK - 1)]
+        z = [keep.tile([P, S], F32, name="z%d" % t) for t in range(PACK)]
         z_grouped = keep.tile([P, S, PACK], BF16, name="z_grouped", align_bytes=64)
+        a, b, nb = {}, {}, {}
 
-        def fetch(t):
-            nc.vector.tensor_copy(out=b[t][:], in_=y[t][:].indirect(lb_sb[:]))
+        def fetch_a(t):
+            a[t] = keep.tile([P, V], F32, name="a", tag="a%d" % (t % 2))
             nc.vector.tensor_copy(out=a[t][:], in_=y[t][:].indirect(la_sb[:]))
+
+        def fetch_b(t):
+            b[t] = keep.tile([P, V], F32, name="b", tag="b%d" % (t % 2), align_bytes=64)
+            nc.vector.tensor_copy(out=b[t][:], in_=y[t][:].indirect(lb_sb[:]))
+            nb[t] = keep.tile([P, V], F32, name="nb%d" % t)
             nc.scalar.activation(out=nb[t][:], in_=b[t][:], func=COPY, scale=-1.0)
 
         def put_sum(t):
@@ -109,32 +112,35 @@ def tile_picked_haarinp_none_p_kernel(tc, x_words, x_scales, w1, w2, offs, la, l
         def round_scalar(t, c0, c1):
             nc.scalar.copy(out=z_grouped[:, c0:c1, t], in_=z[t][:, c0:c1])
 
-        fetch(0)
-        fetch(1)
+        fetch_b(0)
+        fetch_a(0)
+        fetch_b(1)
+        fetch_a(1)
         put_sum(0)
         put_sum(1)
         put_diff(0)
-        fetch(2)
+        put_diff(1)
 
-        w2_grouped = keep.tile([P, N * PACK], BF16, name="w2_grouped", tag="shared", align_bytes=64)
+        w2_grouped = keep.tile([P, N * PACK], BF16, name="w2_grouped", align_bytes=64)
         dst2 = w2_grouped[:].rearrange("p (c i j) -> p c j i", i=4, j=PACK)
         src2 = w2_raw[:].rearrange("p j (c i) -> p c j i", i=4)
         for piece in range(4):
             nc.scalar.copy(out=dst2[:, piece * 32 : (piece + 1) * 32], in_=src2[:, piece * 32 : (piece + 1) * 32])
         w2_codes = keep.tile([P, N], U32, name="w2_codes", align_bytes=64)
-        w2_sc = keep.tile([P, N], U8, name="w2_sc", align_bytes=64)
 
-        put_sum(2)
-        put_diff(1)
-        fetch(3)
+        fetch_b(2)
+        fetch_b(3)
+        fetch_a(2)
+        fetch_a(3)
         round_scalar(0, 0, S)
         round_scalar(1, 0, S)
-        nc.vector.quantize_mx(out=w2_codes[:].bitcast(FP8X4), scales=w2_sc[:], in_=w2_grouped[:])
-        z.append(keep.tile([P, S], F32, name="z3", tag="shared", align_bytes=64))
+        put_sum(2)
         put_sum(3)
         put_diff(2)
         put_diff(3)
         round_scalar(2, 0, S)
+        w2_sc = keep.tile([P, N], U8, name="w2_sc", tag="b1", align_bytes=64)
+        nc.vector.quantize_mx(out=w2_codes[:].bitcast(FP8X4), scales=w2_sc[:], in_=w2_grouped[:])
 
         z_codes = keep.tile([P, S], U32, name="z_codes", align_bytes=64)
         z_sc = keep.tile([P, S], U8, name="z_sc", align_bytes=64)

@@ -33,21 +33,21 @@ def tile_picked_haarinp_none_p_kernel(tc, x_words, x_scales, w1, w2, offs, la, l
         lb_sb = lists.tile([P, V // 16], U16, name="lb_sb")
 
         w1_raw = keep.tile([P, PACK, H], F32, name="w1_raw")
-        x_table = keep.tile([P, T], I32, name="x_table")
+        x_table = keep.tile([P, T], I32, name="x_table", tag="word_rows", align_bytes=64)
         s_table = keep.tile([P, T], U8, name="s_table", tag="scale_rows", align_bytes=64)
         w2_raw = keep.tile([P, PACK, N], F32, name="w2_raw")
 
         nc.vector.memset(s_table[:].bitcast(I32), 0)
-        nc.sync.dma_start(offs_sb[:], offs)
         nc.sync.dma_start(out=w1_raw[:], in_=w1.rearrange("(p j) c -> p j c", j=PACK))
+        for r in range(4):
+            nc.sync.dma_start(
+                out=s_table[r:P:32, :].bitcast(I32),
+                in_=x_scales[0, r:16:4, :].bitcast(I32),
+            )
+        nc.sync.dma_start(offs_sb[:], offs)
+        nc.sync.dma_start(out=x_table[:], in_=x_words[0].rearrange("p n t -> p (n t)").bitcast(I32))
         nc.sync.dma_start(la_sb[:], la)
         nc.sync.dma_start(lb_sb[:], lb)
-        for q in range(4):
-            nc.sync.dma_start(
-                out=s_table[32 * q : 32 * q + 4, :].bitcast(I32),
-                in_=x_scales[0, 4 * q : 4 * q + 4, :].bitcast(I32),
-            )
-        nc.sync.dma_start(out=x_table[:], in_=x_words[0].rearrange("p n t -> p (n t)").bitcast(I32))
         nc.sync.dma_start(out=w2_raw[:], in_=w2.rearrange("(p j) c -> p j c", j=PACK))
 
         w1_grouped = keep.tile([P, PACK * H], BF16, name="w1_grouped", align_bytes=64)
@@ -58,9 +58,9 @@ def tile_picked_haarinp_none_p_kernel(tc, x_words, x_scales, w1, w2, offs, la, l
         x_sc = keep.tile([P, S], U8, name="x_sc", align_bytes=64)
         nc.vector.tensor_copy(out=x_sc[:], in_=s_table[:].indirect(offs_sb[:]))
 
-        w1_codes = keep.tile([P, H], U32, name="w1_codes", tag="scale_rows", align_bytes=64)
         w1_sc = keep.tile([P, H], U8, name="w1_sc", align_bytes=64)
-        nc.vector.quantize_mx(out=w1_codes[:].bitcast(FP8X4), scales=w1_sc[:], in_=w1_grouped[:])
+        w1_first = keep.tile([P, P], U32, name="w1_first", tag="scale_rows", align_bytes=64)
+        nc.vector.quantize_mx(out=w1_first[:].bitcast(FP8X4), scales=w1_sc[:, :P], in_=w1_grouped[:, : PACK * P])
 
         x_codes = keep.tile([P, S], U32, name="x_codes", align_bytes=64)
         for h in range(2):
@@ -69,13 +69,18 @@ def tile_picked_haarinp_none_p_kernel(tc, x_words, x_scales, w1, w2, offs, la, l
                 in_=x_table[:].bitcast(U32).indirect(offs_sb[:, h * HALF // 16 : (h + 1) * HALF // 16]),
             )
 
+        w1_rest = keep.tile([P, H - P], U32, name="w1_rest", tag="word_rows", align_bytes=64)
+        nc.vector.quantize_mx(out=w1_rest[:, :P].bitcast(FP8X4), scales=w1_sc[:, P : 2 * P], in_=w1_grouped[:, PACK * P : 2 * PACK * P])
+        nc.vector.quantize_mx(out=w1_rest[:, P:].bitcast(FP8X4), scales=w1_sc[:, 2 * P :], in_=w1_grouped[:, 2 * PACK * P :])
+        w1_codes = [w1_first[:]] + [w1_rest[:, t * P : (t + 1) * P] for t in range(PACK - 1)]
+
         y = [keep.tile([P, S], F32, name="y%d" % t) for t in range(PACK)]
 
         def first_product(t, c0, c1):
             acc = psum.tile([P, c1 - c0], F32, name="acc", tag="bank")
             nc.tensor.matmul_mx(
                 out=acc[:],
-                lhsT=w1_codes[:, t * P : (t + 1) * P].bitcast(FP8X4),
+                lhsT=w1_codes[t].bitcast(FP8X4),
                 lhsT_scale=w1_sc[:, t * P : (t + 1) * P],
                 rhs=x_codes[:, c0:c1].bitcast(FP8X4),
                 rhs_scale=x_sc[:, c0:c1],
@@ -171,7 +176,7 @@ def tile_picked_haarinp_none_p_kernel(tc, x_words, x_scales, w1, w2, offs, la, l
                         stop=True,
                     )
                 res = keep.tile([P, per_bank, width], F32, name="res%d" % bank)
-                if bank >= 3 and bank % 2 == 1:
+                if bank % 2 == 0:
                     nc.scalar.copy(out=res[:], in_=acc[:])
                 else:
                     nc.vector.tensor_copy(out=res[:], in_=acc[:])

@@ -14,11 +14,12 @@ U8 = mybir.dt.uint8
 FP8X4 = mybir.dt.float8_e4m3fn_x4
 COPY = mybir.ActivationFunctionType.Copy
 ADD = mybir.AluOpType.add
+MULT = mybir.AluOpType.mult
 
 P = 128
 PACK = 4
 HALF = S // 2
-W1_SCALAR_M = 72
+PLANE_ORDER = (0, 2, 3, 1)
 
 
 def tile_picked_haarinp_none_p_kernel(tc, x_words, x_scales, w1, w2, offs, la, lb, out):
@@ -35,87 +36,108 @@ def tile_picked_haarinp_none_p_kernel(tc, x_words, x_scales, w1, w2, offs, la, l
         w1_raw = keep.tile([P, PACK, H], F32, name="w1_raw")
         x_table = keep.tile([P, T], I32, name="x_table", tag="word_rows", align_bytes=64)
         s_table = keep.tile([P, T], U8, name="s_table", tag="scale_rows", align_bytes=64)
-        w2_raw = keep.tile([P, PACK, N], F32, name="w2_raw")
+        x_sc = keep.tile([P, S], U8, name="x_sc", align_bytes=64)
 
         nc.vector.memset(s_table[:].bitcast(I32), 0)
-        nc.sync.dma_start(out=w1_raw[:], in_=w1.rearrange("(p j) c -> p j c", j=PACK))
-        for r in range(4):
-            nc.sync.dma_start(
-                out=s_table[r:P:32, :].bitcast(I32),
-                in_=x_scales[0, r:16:4, :].bitcast(I32),
-            )
+        nc.vector.memset(x_sc[:].bitcast(I32), 0)
+        factor = keep.tile([P, 1], F32, name="factor", tag="z0")
+        nc.vector.memset(factor[:], 0.75)
+        w1_rows = w1.rearrange("(p j) c -> p j c", j=PACK)
+        nc.sync.dma_start(out=w1_raw[:, :2], in_=w1_rows[:, :2])
+        nc.sync.dma_start(out=s_table[32:96:4, :].bitcast(I32), in_=x_scales[0].bitcast(I32))
         nc.sync.dma_start(offs_sb[:], offs)
+        nc.sync.dma_start(out=w1_raw[:, 2:], in_=w1_rows[:, 2:])
         nc.sync.dma_start(out=x_table[:], in_=x_words[0].rearrange("p n t -> p (n t)").bitcast(I32))
         nc.sync.dma_start(la_sb[:], la)
         nc.sync.dma_start(lb_sb[:], lb)
+
+
+        s_picked = keep.tile([P, S], U8, name="s_picked", tag="w2_raw", align_bytes=64)
+        nc.vector.tensor_copy(out=s_picked[:], in_=s_table[:].indirect(offs_sb[:]))
+        for r in range(4):
+            nc.scalar.dma_start(out=x_sc[r:P:32, :].bitcast(I32), in_=s_picked[32 + 4 * r : 96 : 16, :].bitcast(I32))
+        w2_raw = keep.tile([P, PACK, N], F32, name="w2_raw", tag="w2_raw", align_bytes=64)
         nc.sync.dma_start(out=w2_raw[:], in_=w2.rearrange("(p j) c -> p j c", j=PACK))
 
         w1_grouped = keep.tile([P, PACK * H], BF16, name="w1_grouped", align_bytes=64)
         dst = w1_grouped[:].rearrange("p (t m j) -> p m j t", t=PACK, j=PACK)
         src = w1_raw[:].rearrange("p j (m t) -> p m j t", t=PACK)
-        nc.scalar.activation(out=dst[:, :W1_SCALAR_M], in_=src[:, :W1_SCALAR_M], func=COPY)
-        nc.vector.tensor_copy(out=dst[:, W1_SCALAR_M:], in_=src[:, W1_SCALAR_M:])
-        x_sc = keep.tile([P, S], U8, name="x_sc", align_bytes=64)
-        nc.vector.tensor_copy(out=x_sc[:], in_=s_table[:].indirect(offs_sb[:]))
-
-        w1_sc = keep.tile([P, H], U8, name="w1_sc", align_bytes=64)
-        w1_first = keep.tile([P, P], U32, name="w1_first", tag="scale_rows", align_bytes=64)
-        nc.vector.quantize_mx(out=w1_first[:].bitcast(FP8X4), scales=w1_sc[:, :P], in_=w1_grouped[:, : PACK * P])
+        nc.vector.tensor_copy(out=dst, in_=src)
 
         x_codes = keep.tile([P, S], U32, name="x_codes", align_bytes=64)
-        for h in range(2):
-            nc.vector.tensor_copy(
-                out=x_codes[:, h * HALF : (h + 1) * HALF],
-                in_=x_table[:].bitcast(U32).indirect(offs_sb[:, h * HALF // 16 : (h + 1) * HALF // 16]),
-            )
+        w1_codes, w1_sc = {}, {}
 
-        w1_rest = keep.tile([P, H - P], U32, name="w1_rest", tag="word_rows", align_bytes=64)
-        nc.vector.quantize_mx(out=w1_rest[:, :P].bitcast(FP8X4), scales=w1_sc[:, P : 2 * P], in_=w1_grouped[:, PACK * P : 2 * PACK * P])
-        nc.vector.quantize_mx(out=w1_rest[:, P:].bitcast(FP8X4), scales=w1_sc[:, 2 * P :], in_=w1_grouped[:, 2 * PACK * P :])
-        w1_codes = [w1_first[:]] + [w1_rest[:, t * P : (t + 1) * P] for t in range(PACK - 1)]
+        def quantize_w1(n, tag):
+            t = PLANE_ORDER[n]
+            w1_codes[n] = keep.tile([P, P], U32, name="w1_codes", tag=tag, align_bytes=64)
+            w1_sc[n] = keep.tile([P, P], U8, name="w1_sc%d" % n, align_bytes=64)
+            nc.vector.quantize_mx(out=w1_codes[n][:].bitcast(FP8X4), scales=w1_sc[n][:], in_=w1_grouped[:, t * H : (t + 1) * H])
 
-        y = [keep.tile([P, S], F32, name="y%d" % t) for t in range(PACK)]
+        y = [keep.tile([P, S], F32, name="y%d" % n) for n in range(PACK)]
 
-        def first_product(t, c0, c1):
+        def first_product(n, c0, c1):
             acc = psum.tile([P, c1 - c0], F32, name="acc", tag="bank")
             nc.tensor.matmul_mx(
                 out=acc[:],
-                lhsT=w1_codes[t].bitcast(FP8X4),
-                lhsT_scale=w1_sc[:, t * P : (t + 1) * P],
+                lhsT=w1_codes[n][:].bitcast(FP8X4),
+                lhsT_scale=w1_sc[n][:],
                 rhs=x_codes[:, c0:c1].bitcast(FP8X4),
                 rhs_scale=x_sc[:, c0:c1],
                 start=True,
                 stop=True,
             )
-            nc.scalar.activation(out=y[t][:, c0:c1], in_=acc[:], func=COPY, scale=0.75)
+            return acc
 
-        first_product(0, 0, HALF)
-        first_product(0, HALF, S)
-        for t in range(1, PACK):
-            first_product(t, 0, S)
+        def empty_scalar(n, c0, c1, scale=0.75):
+            acc = first_product(n, c0, c1)
+            nc.scalar.activation(out=y[n][:, c0:c1], in_=acc[:], func=COPY, scale=scale)
 
-        z = [keep.tile([P, S], F32, name="z%d" % t) for t in range(PACK)]
+        def empty_vector(n, c0, c1):
+            acc = first_product(n, c0, c1)
+            nc.vector.tensor_scalar(out=y[n][:, c0:c1], in0=acc[:], scalar1=0.75, scalar2=None, op0=MULT)
+
+        quantize_w1(0, "w1_codes0")
+        quantize_w1(1, "w1_codes1")
+        for h in range(2):
+            nc.vector.tensor_copy(
+                out=x_codes[:, h * HALF : (h + 1) * HALF],
+                in_=x_table[:].bitcast(U32).indirect(offs_sb[:, h * HALF // 16 : (h + 1) * HALF // 16]),
+            )
+        quantize_w1(2, "w1_codes2")
+        quantize_w1(3, "w1_codes3")
+        empty_scalar(0, 0, HALF)
+        empty_scalar(1, 0, HALF)
+        empty_vector(0, HALF, HALF + P)
+        empty_vector(0, HALF + P, S)
+        empty_scalar(1, HALF, S, factor[:])
+        for n in range(2, PACK):
+            empty_scalar(n, 0, S)
+
+        z = [keep.tile([P, S], F32, name="z%d" % n, tag="z%d" % n) for n in range(PACK)]
         z_grouped = keep.tile([P, S, PACK], BF16, name="z_grouped", align_bytes=64)
         a, b, nb = {}, {}, {}
 
-        def fetch_a(t):
-            a[t] = keep.tile([P, V], F32, name="a", tag="a%d" % (t % 2))
-            nc.vector.tensor_copy(out=a[t][:], in_=y[t][:].indirect(la_sb[:]))
+        def fetch_a(n):
+            a[n] = keep.tile([P, V], F32, name="a", tag="a%d" % (n % 2), align_bytes=64)
+            nc.vector.tensor_copy(out=a[n][:], in_=y[n][:].indirect(la_sb[:]))
 
-        def fetch_b(t):
-            b[t] = keep.tile([P, V], F32, name="b", tag="b%d" % (t % 2), align_bytes=64)
-            nc.vector.tensor_copy(out=b[t][:], in_=y[t][:].indirect(lb_sb[:]))
-            nb[t] = keep.tile([P, V], F32, name="nb%d" % t)
-            nc.scalar.activation(out=nb[t][:], in_=b[t][:], func=COPY, scale=-1.0)
+        def fetch_b(n):
+            b[n] = keep.tile([P, V], F32, name="b", tag="b%d" % (n % 2), align_bytes=64)
+            nc.vector.tensor_copy(out=b[n][:], in_=y[n][:].indirect(lb_sb[:]))
+            nb[n] = keep.tile([P, V], F32, name="nb%d" % n)
+            nc.scalar.activation(out=nb[n][:], in_=b[n][:], func=COPY, scale=-1.0)
 
-        def put_sum(t):
-            nc.vector.tensor_tensor(z[t][:].indirect(la_sb[:]), a[t][:], b[t][:], ADD)
+        def put_sum(n):
+            nc.vector.tensor_tensor(z[n][:].indirect(la_sb[:]), a[n][:], b[n][:], ADD)
 
-        def put_diff(t):
-            nc.vector.tensor_tensor(z[t][:].indirect(lb_sb[:]), a[t][:], nb[t][:], ADD)
+        def put_diff(n):
+            nc.vector.tensor_tensor(z[n][:].indirect(lb_sb[:]), a[n][:], nb[n][:], ADD)
 
-        def round_scalar(t, c0, c1):
-            nc.scalar.copy(out=z_grouped[:, c0:c1, t], in_=z[t][:, c0:c1])
+        def round_scalar(n, c0, c1):
+            nc.scalar.copy(out=z_grouped[:, c0:c1, PLANE_ORDER[n]], in_=z[n][:, c0:c1])
+
+        def round_vector(n, c0, c1):
+            nc.vector.tensor_copy(out=z_grouped[:, c0:c1, PLANE_ORDER[n]], in_=z[n][:, c0:c1])
 
         fetch_b(0)
         fetch_a(0)
@@ -131,54 +153,70 @@ def tile_picked_haarinp_none_p_kernel(tc, x_words, x_scales, w1, w2, offs, la, l
         src2 = w2_raw[:].rearrange("p j (c i) -> p c j i", i=4)
         for piece in range(4):
             nc.scalar.copy(out=dst2[:, piece * 32 : (piece + 1) * 32], in_=src2[:, piece * 32 : (piece + 1) * 32])
-        w2_codes = keep.tile([P, N], U32, name="w2_codes", align_bytes=64)
 
+        round_scalar(0, 0, S)
         fetch_b(2)
         fetch_b(3)
         fetch_a(2)
         fetch_a(3)
-        round_scalar(0, 0, S)
         round_scalar(1, 0, S)
         put_sum(2)
         put_sum(3)
         put_diff(2)
         put_diff(3)
-        round_scalar(2, 0, S)
-        w2_sc = keep.tile([P, N], U8, name="w2_sc", tag="b1", align_bytes=64)
-        nc.vector.quantize_mx(out=w2_codes[:].bitcast(FP8X4), scales=w2_sc[:], in_=w2_grouped[:])
+        round_scalar(2, 0, HALF)
+        round_scalar(2, HALF, S)
 
+        w2_codes = keep.tile([P, N], U32, name="w2_codes", align_bytes=64)
+        w2_sc = keep.tile([P, N], U8, name="w2_sc", tag="a0", align_bytes=64)
         z_codes = keep.tile([P, S], U32, name="z_codes", align_bytes=64)
         z_sc = keep.tile([P, S], U8, name="z_sc", align_bytes=64)
-        out_blocks = out.rearrange("(u p) c -> p u c", p=P)
-        chunks = [(0, 128), (128, 256), (256, 512)]
-        for c0, c1 in chunks:
-            round_scalar(3, c0, c1)
+
+        def quantize_w2(m0, m1):
+            nc.vector.quantize_mx(out=w2_codes[:, m0:m1].bitcast(FP8X4), scales=w2_sc[:, m0:m1], in_=w2_grouped[:, PACK * m0 : PACK * m1])
+
+        def quantize_z(c0, c1):
             nc.vector.quantize_mx(
                 out=z_codes[:, c0:c1].bitcast(FP8X4),
                 scales=z_sc[:, c0:c1],
                 in_=z_grouped[:, c0:c1, :].rearrange("p c t -> p (c t)"),
             )
-        bank = 0
-        for c0, c1 in chunks:
-            width = c1 - c0
-            per_bank = HALF // width
-            for u0 in range(0, N // P, per_bank):
-                acc = psum.tile([P, per_bank, width], F32, name="acc", tag="bank")
-                for du in range(per_bank):
-                    rows = slice((u0 + du) * P, (u0 + du + 1) * P)
-                    nc.tensor.matmul_mx(
-                        out=acc[:, du, :],
-                        lhsT=w2_codes[:, rows].bitcast(FP8X4),
-                        lhsT_scale=w2_sc[:, rows],
-                        rhs=z_codes[:, c0:c1].bitcast(FP8X4),
-                        rhs_scale=z_sc[:, c0:c1],
-                        start=True,
-                        stop=True,
-                    )
-                res = keep.tile([P, per_bank, width], F32, name="res%d" % bank)
-                if bank % 2 == 0:
-                    nc.scalar.copy(out=res[:], in_=acc[:])
-                else:
-                    nc.vector.tensor_copy(out=res[:], in_=acc[:])
-                nc.sync.dma_start(out=out_blocks[:, u0 : u0 + per_bank, c0:c1], in_=res[:])
-                bank = bank + 1
+
+        out_blocks = out.rearrange("(u p) c -> p u c", p=P)
+
+        def second_product(engine, u0, u1, c0, c1):
+            acc = psum.tile([P, u1 - u0, c1 - c0], F32, name="acc", tag="bank")
+            for u in range(u0, u1):
+                rows = slice(u * P, (u + 1) * P)
+                nc.tensor.matmul_mx(
+                    out=acc[:, u - u0, :],
+                    lhsT=w2_codes[:, rows].bitcast(FP8X4),
+                    lhsT_scale=w2_sc[:, rows],
+                    rhs=z_codes[:, c0:c1].bitcast(FP8X4),
+                    rhs_scale=z_sc[:, c0:c1],
+                    start=True,
+                    stop=True,
+                )
+            res = keep.tile([P, u1 - u0, c1 - c0], F32, name="res%d_%d" % (u0, c0))
+            if engine == "scalar":
+                nc.scalar.copy(out=res[:], in_=acc[:])
+            else:
+                nc.vector.tensor_copy(out=res[:], in_=acc[:])
+            nc.sync.dma_start(out=out_blocks[:, u0:u1, c0:c1], in_=res[:])
+
+        quantize_w2(0, P)
+        round_vector(3, 0, P)
+        round_scalar(3, P, HALF)
+        round_scalar(3, HALF, S)
+        quantize_w2(P, 2 * P)
+        quantize_z(0, P)
+        quantize_w2(2 * P, N)
+        quantize_z(P, HALF)
+        second_product("vector", 0, 1, 0, P)
+        second_product("scalar", 1, 2, 0, P)
+        quantize_z(HALF, S)
+        second_product("scalar", 2, 4, 0, P)
+        second_product("vector", 0, 2, P, HALF)
+        second_product("scalar", 2, 4, P, HALF)
+        for u in range(N // P):
+            second_product("vector" if u % 2 == 0 else "scalar", u, u + 1, HALF, S)

@@ -41,7 +41,9 @@ def tile_picked_haarinp_none_p_kernel(tc, x_words, x_scales, w1, w2, offs, la, l
         nc.vector.memset(s_table[:].bitcast(I32), 0)
         nc.vector.memset(x_sc[:].bitcast(I32), 0)
         factor = keep.tile([P, 1], F32, name="factor", tag="z0")
-        nc.vector.memset(factor[:], 0.75)
+        one = keep.tile([P, 1], F32, name="one")
+        nc.vector.memset(one[:], 1.0)
+        nc.scalar.activation(out=factor[:], in_=one[:], func=COPY, scale=0.75)
         w1_rows = w1.rearrange("(p j) c -> p j c", j=PACK)
         nc.sync.dma_start(out=w1_raw[:, :2], in_=w1_rows[:, :2])
         nc.sync.dma_start(out=s_table[32:96:4, :].bitcast(I32), in_=x_scales[0].bitcast(I32))
@@ -60,9 +62,10 @@ def tile_picked_haarinp_none_p_kernel(tc, x_words, x_scales, w1, w2, offs, la, l
         nc.sync.dma_start(out=w2_raw[:], in_=w2.rearrange("(p j) c -> p j c", j=PACK))
 
         w1_grouped = keep.tile([P, PACK * H], BF16, name="w1_grouped", align_bytes=64)
-        dst = w1_grouped[:].rearrange("p (t m j) -> p m j t", t=PACK, j=PACK)
-        src = w1_raw[:].rearrange("p j (m t) -> p m j t", t=PACK)
-        nc.vector.tensor_copy(out=dst, in_=src)
+        dst = w1_grouped[:].rearrange("p (a b m j) -> p b m j a", a=2, b=2, j=PACK)
+        src = w1_raw[:].rearrange("p j (m a b) -> p b m j a", a=2, b=2)
+        nc.vector.tensor_copy(out=dst[:, 0], in_=src[:, 0])
+        nc.scalar.copy(out=dst[:, 1], in_=src[:, 1])
 
         x_codes = keep.tile([P, S], U32, name="x_codes", align_bytes=64)
         w1_codes, w1_sc = {}, {}
@@ -106,10 +109,9 @@ def tile_picked_haarinp_none_p_kernel(tc, x_words, x_scales, w1, w2, offs, la, l
         quantize_w1(2, "w1_codes2")
         quantize_w1(3, "w1_codes3")
         empty_scalar(0, 0, HALF)
-        empty_scalar(1, 0, HALF)
         empty_vector(0, HALF, HALF + P)
-        empty_vector(0, HALF + P, S)
-        empty_scalar(1, HALF, S, factor[:])
+        empty_scalar(0, HALF + P, S)
+        empty_scalar(1, 0, S, factor[:])
         for n in range(2, PACK):
             empty_scalar(n, 0, S)
 

@@ -40,7 +40,7 @@ def tile_picked_haarinp_none_p_kernel(tc, x_words, x_scales, w1, w2, offs, la, l
 
         nc.vector.memset(s_table[:].bitcast(I32), 0)
         nc.vector.memset(x_sc[:].bitcast(I32), 0)
-        factor = keep.tile([P, 1], F32, name="factor", tag="z0")
+        factor = keep.tile([P, 1], F32, name="factor")
         one = keep.tile([P, 1], F32, name="one")
         nc.vector.memset(one[:], 1.0)
         nc.scalar.activation(out=factor[:], in_=one[:], func=COPY, scale=0.75)
@@ -99,33 +99,22 @@ def tile_picked_haarinp_none_p_kernel(tc, x_words, x_scales, w1, w2, offs, la, l
             acc = first_product(n, c0, c1)
             nc.vector.tensor_scalar(out=y[n][:, c0:c1], in0=acc[:], scalar1=0.75, scalar2=None, op0=MULT)
 
-        quantize_w1(0, "w1_codes0")
-        quantize_w1(1, "w1_codes1")
-        for h in range(2):
-            nc.vector.tensor_copy(
-                out=x_codes[:, h * HALF : (h + 1) * HALF],
-                in_=x_table[:].bitcast(U32).indirect(offs_sb[:, h * HALF // 16 : (h + 1) * HALF // 16]),
-            )
-        quantize_w1(2, "w1_codes2")
-        quantize_w1(3, "w1_codes3")
-        empty_scalar(0, 0, HALF)
-        empty_vector(0, HALF, HALF + P)
-        empty_scalar(0, HALF + P, S)
-        empty_scalar(1, 0, S, factor[:])
-        for n in range(2, PACK):
-            empty_scalar(n, 0, S)
-
         z = [keep.tile([P, S], F32, name="z%d" % n, tag="z%d" % n) for n in range(PACK)]
         z_grouped = keep.tile([P, S, PACK], BF16, name="z_grouped", align_bytes=64)
         a, b, nb = {}, {}, {}
 
         def fetch_a(n):
-            a[n] = keep.tile([P, V], F32, name="a", tag="a%d" % (n % 2), align_bytes=64)
-            nc.vector.tensor_copy(out=a[n][:], in_=y[n][:].indirect(la_sb[:]))
+            a[n] = keep.tile([P, V], F32, name="a%d" % n, tag="a%d" % n, align_bytes=64)
+            if n == 0:
+                nc.vector.tensor_copy(out=a[n][:], in_=y[n][:].indirect(la_sb[:]))
+            else:
+                nc.scalar.activation(out=a[n][:], in_=y[n][:].indirect(la_sb[:]), func=COPY)
 
         def fetch_b(n):
-            b[n] = keep.tile([P, V], F32, name="b", tag="b%d" % (n % 2), align_bytes=64)
-            nc.vector.tensor_copy(out=b[n][:], in_=y[n][:].indirect(lb_sb[:]))
+            b[n] = keep.tile([P, V], F32, name="b%d" % n, align_bytes=64)
+            nc.scalar.activation(out=b[n][:], in_=y[n][:].indirect(lb_sb[:]), func=COPY)
+
+        def negate_b(n):
             nb[n] = keep.tile([P, V], F32, name="nb%d" % n)
             nc.scalar.activation(out=nb[n][:], in_=b[n][:], func=COPY, scale=-1.0)
 
@@ -135,20 +124,52 @@ def tile_picked_haarinp_none_p_kernel(tc, x_words, x_scales, w1, w2, offs, la, l
         def put_diff(n):
             nc.vector.tensor_tensor(z[n][:].indirect(lb_sb[:]), a[n][:], nb[n][:], ADD)
 
-        def round_scalar(n, c0, c1):
-            nc.scalar.copy(out=z_grouped[:, c0:c1, PLANE_ORDER[n]], in_=z[n][:, c0:c1])
+        def round_scalar(n, c0, c1, scale=1.0):
+            nc.scalar.activation(out=z_grouped[:, c0:c1, PLANE_ORDER[n]], in_=z[n][:, c0:c1], func=COPY, scale=scale)
 
         def round_vector(n, c0, c1):
-            nc.vector.tensor_copy(out=z_grouped[:, c0:c1, PLANE_ORDER[n]], in_=z[n][:, c0:c1])
+            nc.vector.tensor_scalar(out=z_grouped[:, c0:c1, PLANE_ORDER[n]], in0=z[n][:, c0:c1], scalar1=late_factor[:], scalar2=None, op0=MULT)
 
+        quantize_w1(0, "w1_codes0")
+        quantize_w1(1, "w1_codes1")
+        for h in range(2):
+            nc.vector.tensor_copy(
+                out=x_codes[:, h * HALF : (h + 1) * HALF],
+                in_=x_table[:].bitcast(U32).indirect(offs_sb[:, h * HALF // 16 : (h + 1) * HALF // 16]),
+            )
+        quantize_w1(2, "w1_codes2")
+        quantize_w1(3, "w1_codes3")
+        empty_scalar(0, 0, HALF, factor[:])
+        empty_scalar(1, 0, HALF)
+        empty_vector(0, HALF, HALF + P)
+        empty_scalar(0, HALF + P, S)
         fetch_b(0)
         fetch_a(0)
+        put_sum(0)
+        empty_scalar(1, HALF, S)
+        empty_scalar(2, 0, HALF)
         fetch_b(1)
         fetch_a(1)
-        put_sum(0)
         put_sum(1)
+        negate_b(0)
         put_diff(0)
+        negate_b(1)
         put_diff(1)
+        pair = keep.tile([P, 2, S], F32, name="pair", tag="pair")
+        for n in range(2):
+            nc.sync.dma_start(out=pair[:, n, :], in_=z[n][:])
+        empty_scalar(2, HALF, S)
+        empty_scalar(3, 0, S, 1.0)
+        fetch_b(2)
+        fetch_a(2)
+        put_sum(2)
+        fetch_b(3)
+        fetch_a(3)
+        put_sum(3)
+        negate_b(2)
+        put_diff(2)
+        negate_b(3)
+        put_diff(3)
 
         w2_grouped = keep.tile([P, N * PACK], BF16, name="w2_grouped", align_bytes=64)
         dst2 = w2_grouped[:].rearrange("p (c i j) -> p c j i", i=4, j=PACK)
@@ -156,21 +177,14 @@ def tile_picked_haarinp_none_p_kernel(tc, x_words, x_scales, w1, w2, offs, la, l
         for piece in range(4):
             nc.scalar.copy(out=dst2[:, piece * 32 : (piece + 1) * 32], in_=src2[:, piece * 32 : (piece + 1) * 32])
 
-        round_scalar(0, 0, S)
-        fetch_b(2)
-        fetch_b(3)
-        fetch_a(2)
-        fetch_a(3)
-        round_scalar(1, 0, S)
-        put_sum(2)
-        put_sum(3)
-        put_diff(2)
-        put_diff(3)
+        nc.scalar.copy(out=z_grouped[:, :, 0:PACK:2], in_=pair[:].rearrange("p n c -> p c n"))
+        late_factor = keep.tile([P, 1], F32, name="late_factor", tag="pair")
+        nc.scalar.activation(out=late_factor[:], in_=one[:], func=COPY, scale=0.75)
         round_scalar(2, 0, HALF)
         round_scalar(2, HALF, S)
 
         w2_codes = keep.tile([P, N], U32, name="w2_codes", align_bytes=64)
-        w2_sc = keep.tile([P, N], U8, name="w2_sc", tag="a0", align_bytes=64)
+        w2_sc = keep.tile([P, N], U8, name="w2_sc", tag="a3", align_bytes=64)
         z_codes = keep.tile([P, S], U32, name="z_codes", align_bytes=64)
         z_sc = keep.tile([P, S], U8, name="z_sc", align_bytes=64)
 
@@ -208,8 +222,8 @@ def tile_picked_haarinp_none_p_kernel(tc, x_words, x_scales, w1, w2, offs, la, l
 
         quantize_w2(0, P)
         round_vector(3, 0, P)
-        round_scalar(3, P, HALF)
-        round_scalar(3, HALF, S)
+        round_scalar(3, P, HALF, 0.75)
+        round_scalar(3, HALF, S, 0.75)
         quantize_w2(P, 2 * P)
         quantize_z(0, P)
         quantize_w2(2 * P, N)

@@ -76,7 +76,7 @@ def tile_picked_haarinp_none_p_kernel(tc, x_words, x_scales, w1, w2, offs, la, l
             w1_sc[n] = keep.tile([P, P], U8, name="w1_sc%d" % n, align_bytes=64)
             nc.vector.quantize_mx(out=w1_codes[n][:].bitcast(FP8X4), scales=w1_sc[n][:], in_=w1_grouped[:, t * H : (t + 1) * H])
 
-        y = [keep.tile([P, S], F32, name="y%d" % n) for n in range(PACK)]
+        y = [keep.tile([P, S], F32, name="y%d" % n, tag="y%d" % n, align_bytes=64) for n in range(PACK)]
 
         def first_product(n, c0, c1):
             acc = psum.tile([P, c1 - c0], F32, name="acc", tag="bank")
@@ -101,28 +101,28 @@ def tile_picked_haarinp_none_p_kernel(tc, x_words, x_scales, w1, w2, offs, la, l
 
         z = [keep.tile([P, S], F32, name="z%d" % n, tag="z%d" % n) for n in range(PACK)]
         z_grouped = keep.tile([P, S, PACK], BF16, name="z_grouped", align_bytes=64)
-        a, b, nb = {}, {}, {}
+        a = [keep.tile([P, V], F32, name="a%d" % n, tag="a%d" % n, align_bytes=64) for n in range(PACK)]
+        b = keep.tile([P, PACK, V], F32, name="b")
+        nb = {}
 
         def fetch_a(n):
-            a[n] = keep.tile([P, V], F32, name="a%d" % n, tag="a%d" % n, align_bytes=64)
             if n == 0:
                 nc.vector.tensor_copy(out=a[n][:], in_=y[n][:].indirect(la_sb[:]))
             else:
                 nc.scalar.activation(out=a[n][:], in_=y[n][:].indirect(la_sb[:]), func=COPY)
 
         def fetch_b(n):
-            b[n] = keep.tile([P, V], F32, name="b%d" % n, align_bytes=64)
-            nc.scalar.activation(out=b[n][:], in_=y[n][:].indirect(lb_sb[:]), func=COPY)
+            nc.scalar.activation(out=b[:, n, :], in_=y[n][:].indirect(lb_sb[:]), func=COPY)
 
-        def negate_b(n):
-            nb[n] = keep.tile([P, V], F32, name="nb%d" % n)
-            nc.scalar.activation(out=nb[n][:], in_=b[n][:], func=COPY, scale=-1.0)
+        def negate_pair(n):
+            nb[n] = keep.tile([P, 2, V], F32, name="nb", tag="y%d" % (n + 1), align_bytes=64)
+            nc.scalar.activation(out=nb[n][:], in_=b[:, n : n + 2, :], func=COPY, scale=-1.0)
 
         def put_sum(n):
-            nc.vector.tensor_tensor(z[n][:].indirect(la_sb[:]), a[n][:], b[n][:], ADD)
+            nc.vector.tensor_tensor(z[n][:].indirect(la_sb[:]), a[n][:], b[:, n, :], ADD)
 
         def put_diff(n):
-            nc.vector.tensor_tensor(z[n][:].indirect(lb_sb[:]), a[n][:], nb[n][:], ADD)
+            nc.vector.tensor_tensor(z[n][:].indirect(lb_sb[:]), a[n][:], nb[n - n % 2][:, n % 2, :], ADD)
 
         def round_scalar(n, c0, c1, scale=1.0):
             nc.scalar.activation(out=z_grouped[:, c0:c1, PLANE_ORDER[n]], in_=z[n][:, c0:c1], func=COPY, scale=scale)
@@ -140,9 +140,10 @@ def tile_picked_haarinp_none_p_kernel(tc, x_words, x_scales, w1, w2, offs, la, l
         quantize_w1(2, "w1_codes2")
         quantize_w1(3, "w1_codes3")
         empty_scalar(0, 0, HALF, factor[:])
-        empty_scalar(1, 0, HALF)
         empty_vector(0, HALF, HALF + P)
         empty_scalar(0, HALF + P, S)
+        empty_vector(1, 0, P)
+        empty_scalar(1, P, HALF)
         fetch_b(0)
         fetch_a(0)
         put_sum(0)
@@ -151,14 +152,13 @@ def tile_picked_haarinp_none_p_kernel(tc, x_words, x_scales, w1, w2, offs, la, l
         fetch_b(1)
         fetch_a(1)
         put_sum(1)
-        negate_b(0)
+        empty_scalar(2, HALF, S)
+        negate_pair(0)
         put_diff(0)
-        negate_b(1)
         put_diff(1)
-        pair = keep.tile([P, 2, S], F32, name="pair", tag="pair")
+        pair = keep.tile([P, 2, S], F32, name="pair", tag="pair", align_bytes=64)
         for n in range(2):
             nc.sync.dma_start(out=pair[:, n, :], in_=z[n][:])
-        empty_scalar(2, HALF, S)
         empty_scalar(3, 0, S, 1.0)
         fetch_b(2)
         fetch_a(2)
@@ -166,10 +166,6 @@ def tile_picked_haarinp_none_p_kernel(tc, x_words, x_scales, w1, w2, offs, la, l
         fetch_b(3)
         fetch_a(3)
         put_sum(3)
-        negate_b(2)
-        put_diff(2)
-        negate_b(3)
-        put_diff(3)
 
         w2_grouped = keep.tile([P, N * PACK], BF16, name="w2_grouped", align_bytes=64)
         dst2 = w2_grouped[:].rearrange("p (c i j) -> p c j i", i=4, j=PACK)
@@ -177,19 +173,24 @@ def tile_picked_haarinp_none_p_kernel(tc, x_words, x_scales, w1, w2, offs, la, l
         for piece in range(4):
             nc.scalar.copy(out=dst2[:, piece * 32 : (piece + 1) * 32], in_=src2[:, piece * 32 : (piece + 1) * 32])
 
+        negate_pair(2)
+        put_diff(2)
+        put_diff(3)
         nc.scalar.copy(out=z_grouped[:, :, 0:PACK:2], in_=pair[:].rearrange("p n c -> p c n"))
-        late_factor = keep.tile([P, 1], F32, name="late_factor", tag="pair")
+        late_factor = keep.tile([P, 1], F32, name="late_factor", tag="pair", align_bytes=64)
         nc.scalar.activation(out=late_factor[:], in_=one[:], func=COPY, scale=0.75)
         round_scalar(2, 0, HALF)
         round_scalar(2, HALF, S)
 
         w2_codes = keep.tile([P, N], U32, name="w2_codes", align_bytes=64)
-        w2_sc = keep.tile([P, N], U8, name="w2_sc", tag="a3", align_bytes=64)
+        w2_sc = {}
         z_codes = keep.tile([P, S], U32, name="z_codes", align_bytes=64)
         z_sc = keep.tile([P, S], U8, name="z_sc", align_bytes=64)
 
-        def quantize_w2(m0, m1):
-            nc.vector.quantize_mx(out=w2_codes[:, m0:m1].bitcast(FP8X4), scales=w2_sc[:, m0:m1], in_=w2_grouped[:, PACK * m0 : PACK * m1])
+        def quantize_w2(half, tag):
+            m0, m1 = half * N // 2, (half + 1) * N // 2
+            w2_sc[half] = keep.tile([P, N // 2], U8, name="w2_sc", tag=tag, align_bytes=64)
+            nc.vector.quantize_mx(out=w2_codes[:, m0:m1].bitcast(FP8X4), scales=w2_sc[half][:], in_=w2_grouped[:, PACK * m0 : PACK * m1])
 
         def quantize_z(c0, c1):
             nc.vector.quantize_mx(
@@ -207,7 +208,7 @@ def tile_picked_haarinp_none_p_kernel(tc, x_words, x_scales, w1, w2, offs, la, l
                 nc.tensor.matmul_mx(
                     out=acc[:, u - u0, :],
                     lhsT=w2_codes[:, rows].bitcast(FP8X4),
-                    lhsT_scale=w2_sc[:, rows],
+                    lhsT_scale=w2_sc[u // 2][:, u % 2 * P : (u % 2 + 1) * P],
                     rhs=z_codes[:, c0:c1].bitcast(FP8X4),
                     rhs_scale=z_sc[:, c0:c1],
                     start=True,
@@ -220,13 +221,12 @@ def tile_picked_haarinp_none_p_kernel(tc, x_words, x_scales, w1, w2, offs, la, l
                 nc.vector.tensor_copy(out=res[:], in_=acc[:])
             nc.sync.dma_start(out=out_blocks[:, u0:u1, c0:c1], in_=res[:])
 
-        quantize_w2(0, P)
+        quantize_w2(0, "a3")
         round_vector(3, 0, P)
         round_scalar(3, P, HALF, 0.75)
         round_scalar(3, HALF, S, 0.75)
-        quantize_w2(P, 2 * P)
         quantize_z(0, P)
-        quantize_w2(2 * P, N)
+        quantize_w2(1, "pair")
         quantize_z(P, HALF)
         second_product("vector", 0, 1, 0, P)
         second_product("scalar", 1, 2, 0, P)

@@ -19,7 +19,9 @@ MULT = mybir.AluOpType.mult
 P = 128
 PACK = 4
 HALF = S // 2
-PLANE_ORDER = (0, 2, 3, 1)
+GAIN = 0.75
+SLOT = (1, 3, 0, 2)
+CHUNKS = ((0, P), (P, HALF), (HALF, S))
 
 
 def tile_picked_haarinp_none_p_kernel(tc, x_words, x_scales, w1, w2, offs, la, lb, out):
@@ -34,16 +36,17 @@ def tile_picked_haarinp_none_p_kernel(tc, x_words, x_scales, w1, w2, offs, la, l
         lb_sb = lists.tile([P, V // 16], U16, name="lb_sb")
 
         w1_raw = keep.tile([P, PACK, H], F32, name="w1_raw")
-        x_table = keep.tile([P, T], I32, name="x_table", tag="word_rows", align_bytes=64)
-        s_table = keep.tile([P, T], U8, name="s_table", tag="scale_rows", align_bytes=64)
+        x_table = keep.tile([P, T], I32, name="x_table", align_bytes=64)
+        s_table = keep.tile([P, T], U8, name="s_table", align_bytes=64)
         x_sc = keep.tile([P, S], U8, name="x_sc", align_bytes=64)
 
         nc.vector.memset(s_table[:].bitcast(I32), 0)
         nc.vector.memset(x_sc[:].bitcast(I32), 0)
-        factor = keep.tile([P, 1], F32, name="factor")
         one = keep.tile([P, 1], F32, name="one")
         nc.vector.memset(one[:], 1.0)
-        nc.scalar.activation(out=factor[:], in_=one[:], func=COPY, scale=0.75)
+        minus = keep.tile([P, 1], F32, name="minus")
+        nc.scalar.activation(out=minus[:], in_=one[:], func=COPY, scale=-1.0)
+
         w1_rows = w1.rearrange("(p j) c -> p j c", j=PACK)
         nc.sync.dma_start(out=w1_raw[:, :2], in_=w1_rows[:, :2])
         nc.sync.dma_start(out=s_table[32:96:4, :].bitcast(I32), in_=x_scales[0].bitcast(I32))
@@ -53,7 +56,6 @@ def tile_picked_haarinp_none_p_kernel(tc, x_words, x_scales, w1, w2, offs, la, l
         nc.sync.dma_start(la_sb[:], la)
         nc.sync.dma_start(lb_sb[:], lb)
 
-
         s_picked = keep.tile([P, S], U8, name="s_picked", tag="w2_raw", align_bytes=64)
         nc.vector.tensor_copy(out=s_picked[:], in_=s_table[:].indirect(offs_sb[:]))
         for r in range(4):
@@ -62,23 +64,25 @@ def tile_picked_haarinp_none_p_kernel(tc, x_words, x_scales, w1, w2, offs, la, l
         nc.sync.dma_start(out=w2_raw[:], in_=w2.rearrange("(p j) c -> p j c", j=PACK))
 
         w1_grouped = keep.tile([P, PACK * H], BF16, name="w1_grouped", align_bytes=64)
-        dst = w1_grouped[:].rearrange("p (a b m j) -> p b m j a", a=2, b=2, j=PACK)
-        src = w1_raw[:].rearrange("p j (m a b) -> p b m j a", a=2, b=2)
-        nc.vector.tensor_copy(out=dst[:, 0], in_=src[:, 0])
-        nc.scalar.copy(out=dst[:, 1], in_=src[:, 1])
+        dst = w1_grouped[:].rearrange("p (a b m j) -> p a m j b", a=2, b=2, j=PACK)
+        src = w1_raw[:].rearrange("p j (m b a) -> p a m j b", a=2, b=2)
+        nc.vector.tensor_copy(out=dst[:, 1], in_=src[:, 1])
+        nc.scalar.copy(out=dst[:, 0], in_=src[:, 0])
 
         x_codes = keep.tile([P, S], U32, name="x_codes", align_bytes=64)
-        w1_codes, w1_sc = {}, {}
+        w1_codes = [keep.tile([P, P], U32, name="w1_codes%d" % n, align_bytes=64) for n in range(PACK)]
+        w1_sc = [keep.tile([P, P], U8, name="w1_sc%d" % n, align_bytes=64) for n in range(PACK)]
 
-        def quantize_w1(n, tag):
-            t = PLANE_ORDER[n]
-            w1_codes[n] = keep.tile([P, P], U32, name="w1_codes", tag=tag, align_bytes=64)
-            w1_sc[n] = keep.tile([P, P], U8, name="w1_sc%d" % n, align_bytes=64)
-            nc.vector.quantize_mx(out=w1_codes[n][:].bitcast(FP8X4), scales=w1_sc[n][:], in_=w1_grouped[:, t * H : (t + 1) * H])
+        def quantize_w1(n):
+            at = (SLOT[n] % 2 * 2 + SLOT[n] // 2) * H
+            nc.vector.quantize_mx(out=w1_codes[n][:].bitcast(FP8X4), scales=w1_sc[n][:], in_=w1_grouped[:, at : at + H])
+
+        def pick_words(c0, c1):
+            nc.vector.tensor_copy(out=x_codes[:, c0:c1], in_=x_table[:].bitcast(U32).indirect(offs_sb[:, c0 // 16 : c1 // 16]))
 
         y = [keep.tile([P, S], F32, name="y%d" % n, tag="y%d" % n, align_bytes=64) for n in range(PACK)]
 
-        def first_product(n, c0, c1):
+        def first_product(engine, n, c0, c1):
             acc = psum.tile([P, c1 - c0], F32, name="acc", tag="bank")
             nc.tensor.matmul_mx(
                 out=acc[:],
@@ -89,98 +93,94 @@ def tile_picked_haarinp_none_p_kernel(tc, x_words, x_scales, w1, w2, offs, la, l
                 start=True,
                 stop=True,
             )
-            return acc
+            if engine == "scalar":
+                nc.scalar.copy(out=y[n][:, c0:c1], in_=acc[:])
+            else:
+                nc.vector.tensor_copy(out=y[n][:, c0:c1], in_=acc[:])
 
-        def empty_scalar(n, c0, c1, scale=0.75):
-            acc = first_product(n, c0, c1)
-            nc.scalar.activation(out=y[n][:, c0:c1], in_=acc[:], func=COPY, scale=scale)
-
-        def empty_vector(n, c0, c1):
-            acc = first_product(n, c0, c1)
-            nc.vector.tensor_scalar(out=y[n][:, c0:c1], in0=acc[:], scalar1=0.75, scalar2=None, op0=MULT)
-
-        z = [keep.tile([P, S], F32, name="z%d" % n, tag="z%d" % n) for n in range(PACK)]
-        z_grouped = keep.tile([P, S, PACK], BF16, name="z_grouped", align_bytes=64)
+        early = [keep.tile([P, S], F32, name="early%d" % n) for n in range(2)]
+        pair = [keep.tile([P, 2 * S], F32, name="pair%d" % n) for n in range(2)]
+        window = early + pair
+        z_grouped = {c0: keep.tile([P, c1 - c0, PACK], BF16, name="z_grouped%d" % c0, align_bytes=64) for c0, c1 in CHUNKS}
         a = [keep.tile([P, V], F32, name="a%d" % n, tag="a%d" % n, align_bytes=64) for n in range(PACK)]
         b = keep.tile([P, PACK, V], F32, name="b")
         nb = {}
 
-        def fetch_a(n):
+        def fetch(n):
+            nc.scalar.activation(out=b[:, n, :], in_=y[n][:].indirect(lb_sb[:]), func=COPY)
             if n == 0:
                 nc.vector.tensor_copy(out=a[n][:], in_=y[n][:].indirect(la_sb[:]))
             else:
                 nc.scalar.activation(out=a[n][:], in_=y[n][:].indirect(la_sb[:]), func=COPY)
 
-        def fetch_b(n):
-            nc.scalar.activation(out=b[:, n, :], in_=y[n][:].indirect(lb_sb[:]), func=COPY)
-
         def negate_pair(n):
             nb[n] = keep.tile([P, 2, V], F32, name="nb", tag="y%d" % (n + 1), align_bytes=64)
-            nc.scalar.activation(out=nb[n][:], in_=b[:, n : n + 2, :], func=COPY, scale=-1.0)
+            nc.scalar.activation(out=nb[n][:], in_=b[:, n : n + 2, :], func=COPY, scale=minus[:])
 
         def put_sum(n):
-            nc.vector.tensor_tensor(z[n][:].indirect(la_sb[:]), a[n][:], b[:, n, :], ADD)
+            nc.vector.tensor_tensor(window[n][:].indirect(la_sb[:]), a[n][:], b[:, n, :], ADD)
 
         def put_diff(n):
-            nc.vector.tensor_tensor(z[n][:].indirect(lb_sb[:]), a[n][:], nb[n - n % 2][:, n % 2, :], ADD)
+            nc.vector.tensor_tensor(window[n][:].indirect(lb_sb[:]), a[n][:], nb[n - n % 2][:, n % 2, :], ADD)
 
-        def round_scalar(n, c0, c1, scale=1.0):
-            nc.scalar.activation(out=z_grouped[:, c0:c1, PLANE_ORDER[n]], in_=z[n][:, c0:c1], func=COPY, scale=scale)
-
-        def round_vector(n, c0, c1):
-            nc.vector.tensor_scalar(out=z_grouped[:, c0:c1, PLANE_ORDER[n]], in0=z[n][:, c0:c1], scalar1=late_factor[:], scalar2=None, op0=MULT)
-
-        quantize_w1(0, "w1_codes0")
-        quantize_w1(1, "w1_codes1")
-        for h in range(2):
-            nc.vector.tensor_copy(
-                out=x_codes[:, h * HALF : (h + 1) * HALF],
-                in_=x_table[:].bitcast(U32).indirect(offs_sb[:, h * HALF // 16 : (h + 1) * HALF // 16]),
-            )
-        quantize_w1(2, "w1_codes2")
-        quantize_w1(3, "w1_codes3")
-        empty_scalar(0, 0, HALF, factor[:])
-        empty_vector(0, HALF, HALF + P)
-        empty_scalar(0, HALF + P, S)
-        empty_vector(1, 0, P)
-        empty_scalar(1, P, HALF)
-        fetch_b(0)
-        fetch_a(0)
-        put_sum(0)
-        empty_scalar(1, HALF, S)
-        empty_scalar(2, 0, HALF)
-        fetch_b(1)
-        fetch_a(1)
-        put_sum(1)
-        empty_scalar(2, HALF, S)
-        negate_pair(0)
-        put_diff(0)
-        put_diff(1)
-        pair = keep.tile([P, 2, S], F32, name="pair", tag="pair", align_bytes=64)
-        for n in range(2):
-            nc.sync.dma_start(out=pair[:, n, :], in_=z[n][:])
-        empty_scalar(3, 0, S, 1.0)
-        fetch_b(2)
-        fetch_a(2)
-        put_sum(2)
-        fetch_b(3)
-        fetch_a(3)
-        put_sum(3)
+        def join(n):
+            nc.scalar.copy(out=pair[n][:, S:], in_=early[n][:])
 
         w2_grouped = keep.tile([P, N * PACK], BF16, name="w2_grouped", align_bytes=64)
         dst2 = w2_grouped[:].rearrange("p (c i j) -> p c j i", i=4, j=PACK)
         src2 = w2_raw[:].rearrange("p j (c i) -> p c j i", i=4)
-        for piece in range(4):
-            nc.scalar.copy(out=dst2[:, piece * 32 : (piece + 1) * 32], in_=src2[:, piece * 32 : (piece + 1) * 32])
 
+        def round_w2(u):
+            nc.scalar.copy(out=dst2[:, u * 32 : (u + 1) * 32], in_=src2[:, u * 32 : (u + 1) * 32])
+
+        quantize_w1(0)
+        quantize_w1(1)
+        pick_words(0, HALF)
+        pick_words(HALF, S)
+        quantize_w1(2)
+        quantize_w1(3)
+        first_product("scalar", 0, 0, HALF)
+        first_product("vector", 0, HALF, HALF + P)
+        first_product("scalar", 0, HALF + P, S)
+        first_product("vector", 1, 0, P)
+        first_product("scalar", 1, P, HALF)
+        fetch(0)
+        put_sum(0)
+        first_product("scalar", 1, HALF, S)
+        first_product("scalar", 2, 0, HALF)
+        fetch(1)
+        put_sum(1)
+        negate_pair(0)
+        put_diff(0)
+        put_diff(1)
+        first_product("scalar", 2, HALF, S)
+        first_product("scalar", 3, 0, S)
+        fetch(2)
+        fetch(3)
+        join(0)
+        put_sum(2)
+        round_w2(0)
+        join(1)
+        put_sum(3)
         negate_pair(2)
         put_diff(2)
         put_diff(3)
-        nc.scalar.copy(out=z_grouped[:, :, 0:PACK:2], in_=pair[:].rearrange("p n c -> p c n"))
-        late_factor = keep.tile([P, 1], F32, name="late_factor", tag="pair", align_bytes=64)
-        nc.scalar.activation(out=late_factor[:], in_=one[:], func=COPY, scale=0.75)
-        round_scalar(2, 0, HALF)
-        round_scalar(2, HALF, S)
+        for u in range(1, PACK):
+            round_w2(u)
+
+        gain = keep.tile([P, 1], F32, name="gain", tag="w2_raw", align_bytes=64)
+        nc.scalar.activation(out=gain[:], in_=one[:], func=COPY, scale=GAIN)
+        first_gain = keep.tile([P, 1], F32, name="first_gain", tag="first_gain", align_bytes=64)
+        nc.scalar.copy(out=first_gain[:], in_=gain[:])
+
+        def round_z(engine, n, c0, c1, scale):
+            src_z = pair[n][:].rearrange("p (h c) -> p c h", h=2)[:, c0:c1, :]
+            at = max(c for c in z_grouped if c <= c0)
+            dst_z = z_grouped[at][:, c0 - at : c1 - at, 2 * n : 2 * n + 2]
+            if engine == "scalar":
+                nc.scalar.activation(out=dst_z, in_=src_z, func=COPY, scale=scale)
+            else:
+                nc.vector.tensor_scalar(out=dst_z, in0=src_z, scalar1=scale, scalar2=None, op0=MULT)
 
         w2_codes = keep.tile([P, N], U32, name="w2_codes", align_bytes=64)
         w2_sc = {}
@@ -196,43 +196,50 @@ def tile_picked_haarinp_none_p_kernel(tc, x_words, x_scales, w1, w2, offs, la, l
             nc.vector.quantize_mx(
                 out=z_codes[:, c0:c1].bitcast(FP8X4),
                 scales=z_sc[:, c0:c1],
-                in_=z_grouped[:, c0:c1, :].rearrange("p c t -> p (c t)"),
+                in_=z_grouped[c0][:].rearrange("p c t -> p (c t)"),
             )
 
         out_blocks = out.rearrange("(u p) c -> p u c", p=P)
 
-        def second_product(engine, u0, u1, c0, c1):
-            acc = psum.tile([P, u1 - u0, c1 - c0], F32, name="acc", tag="bank")
-            for u in range(u0, u1):
-                rows = slice(u * P, (u + 1) * P)
+        def second_product(pieces):
+            u0, u1 = pieces[0][1], pieces[-1][1] + 1
+            s0, s1 = pieces[0][2], pieces[-1][3]
+            res = keep.tile([P, u1 - u0, s1 - s0], F32, name="res%d_%d" % (u0, s0))
+            for engine, u, c0, c1 in pieces:
+                acc = psum.tile([P, c1 - c0], F32, name="acc", tag="bank")
                 nc.tensor.matmul_mx(
-                    out=acc[:, u - u0, :],
-                    lhsT=w2_codes[:, rows].bitcast(FP8X4),
+                    out=acc[:],
+                    lhsT=w2_codes[:, u * P : (u + 1) * P].bitcast(FP8X4),
                     lhsT_scale=w2_sc[u // 2][:, u % 2 * P : (u % 2 + 1) * P],
                     rhs=z_codes[:, c0:c1].bitcast(FP8X4),
                     rhs_scale=z_sc[:, c0:c1],
                     start=True,
                     stop=True,
                 )
-            res = keep.tile([P, u1 - u0, c1 - c0], F32, name="res%d_%d" % (u0, c0))
-            if engine == "scalar":
-                nc.scalar.copy(out=res[:], in_=acc[:])
-            else:
-                nc.vector.tensor_copy(out=res[:], in_=acc[:])
-            nc.sync.dma_start(out=out_blocks[:, u0:u1, c0:c1], in_=res[:])
+                if engine == "scalar":
+                    nc.scalar.copy(out=res[:, u - u0, c0 - s0 : c1 - s0], in_=acc[:])
+                else:
+                    nc.vector.tensor_copy(out=res[:, u - u0, c0 - s0 : c1 - s0], in_=acc[:])
+            nc.sync.dma_start(out=out_blocks[:, u0:u1, s0:s1], in_=res[:])
 
+        round_z("scalar", 0, 0, P, gain[:])
+        round_z("scalar", 0, HALF, S, gain[:])
         quantize_w2(0, "a3")
-        round_vector(3, 0, P)
-        round_scalar(3, P, HALF, 0.75)
-        round_scalar(3, HALF, S, 0.75)
+        round_z("scalar", 1, 0, P, first_gain[:])
+        round_z("scalar", 0, P, HALF, gain[:])
+        round_z("vector", 1, P, HALF, gain[:])
+        round_z("vector", 1, HALF, 3 * P, gain[:])
+        round_z("scalar", 1, 3 * P, S, gain[:])
         quantize_z(0, P)
-        quantize_w2(1, "pair")
+        quantize_w2(1, "first_gain")
         quantize_z(P, HALF)
-        second_product("vector", 0, 1, 0, P)
-        second_product("scalar", 1, 2, 0, P)
         quantize_z(HALF, S)
-        second_product("scalar", 2, 4, 0, P)
-        second_product("vector", 0, 2, P, HALF)
-        second_product("scalar", 2, 4, P, HALF)
-        for u in range(N // P):
-            second_product("vector" if u % 2 == 0 else "scalar", u, u + 1, HALF, S)
+        second_product([("scalar", 0, 0, P)])
+        second_product([("scalar", 1, 0, P)])
+        second_product([("scalar", 2, 0, P), ("vector", 3, 0, P)])
+        second_product([("scalar", 0, P, HALF), ("vector", 1, P, HALF)])
+        second_product([("scalar", 2, P, HALF), ("vector", 3, P, HALF)])
+        second_product([("scalar", 0, HALF, S)])
+        second_product([("vector", 1, HALF, S)])
+        second_product([("scalar", 2, HALF, S)])
+        second_product([("vector", 3, HALF, 3 * P), ("scalar", 3, 3 * P, S)])

@@ -20,6 +20,7 @@ P = 128
 PACK = 4
 HALF = S // 2
 GAIN = 0.75
+BANKS = 8
 SLOT = (1, 3, 0, 2)
 CHUNKS = ((0, P), (P, HALF), (HALF, S))
 
@@ -29,7 +30,7 @@ def tile_picked_haarinp_none_p_kernel(tc, x_words, x_scales, w1, w2, offs, la, l
     with ExitStack() as ctx:
         lists = ctx.enter_context(tc.tile_pool(name="lists", bufs=1))
         keep = ctx.enter_context(tc.tile_pool(name="keep", bufs=1))
-        psum = ctx.enter_context(tc.psum_pool(name="psum", bufs=8))
+        psum = ctx.enter_context(tc.psum_pool(name="psum", bufs=1))
 
         offs_sb = lists.tile([P, S // 16], U16, name="offs_sb")
         la_sb = lists.tile([P, V // 16], U16, name="la_sb")
@@ -82,8 +83,8 @@ def tile_picked_haarinp_none_p_kernel(tc, x_words, x_scales, w1, w2, offs, la, l
 
         y = [keep.tile([P, S], F32, name="y%d" % n, tag="y%d" % n, align_bytes=64) for n in range(PACK)]
 
-        def first_product(engine, n, c0, c1):
-            acc = psum.tile([P, c1 - c0], F32, name="acc", tag="bank")
+        def first_product(engine, n, c0, c1, bank):
+            acc = psum.tile([P, c1 - c0], F32, name="acc", tag="bank%d" % bank)
             nc.tensor.matmul_mx(
                 out=acc[:],
                 lhsT=w1_codes[n][:].bitcast(FP8X4),
@@ -136,25 +137,25 @@ def tile_picked_haarinp_none_p_kernel(tc, x_words, x_scales, w1, w2, offs, la, l
         quantize_w1(0)
         quantize_w1(1)
         pick_words(0, HALF)
-        pick_words(HALF, S)
+        pick_words(HALF, HALF + P)
+        pick_words(HALF + P, S)
         quantize_w1(2)
         quantize_w1(3)
-        first_product("scalar", 0, 0, HALF)
-        first_product("vector", 0, HALF, HALF + P)
-        first_product("scalar", 0, HALF + P, S)
-        first_product("vector", 1, 0, P)
-        first_product("scalar", 1, P, HALF)
+        first_product("scalar", 0, 0, HALF, 0)
+        first_product("vector", 0, HALF, HALF + P, 1)
+        first_product("scalar", 0, HALF + P, S, 2)
         fetch(0)
+        first_product("vector", 1, 0, HALF, 0)
         put_sum(0)
-        first_product("scalar", 1, HALF, S)
-        first_product("scalar", 2, 0, HALF)
+        first_product("scalar", 1, HALF, S, 1)
+        first_product("scalar", 2, 0, HALF, 2)
         fetch(1)
         put_sum(1)
         negate_pair(0)
         put_diff(0)
         put_diff(1)
-        first_product("scalar", 2, HALF, S)
-        first_product("scalar", 3, 0, S)
+        first_product("scalar", 2, HALF, S, 0)
+        first_product("scalar", 3, 0, S, 1)
         fetch(2)
         fetch(3)
         join(0)
@@ -201,12 +202,15 @@ def tile_picked_haarinp_none_p_kernel(tc, x_words, x_scales, w1, w2, offs, la, l
 
         out_blocks = out.rearrange("(u p) c -> p u c", p=P)
 
+        done = []
+
         def second_product(pieces):
             u0, u1 = pieces[0][1], pieces[-1][1] + 1
             s0, s1 = pieces[0][2], pieces[-1][3]
             res = keep.tile([P, u1 - u0, s1 - s0], F32, name="res%d_%d" % (u0, s0))
             for engine, u, c0, c1 in pieces:
-                acc = psum.tile([P, c1 - c0], F32, name="acc", tag="bank")
+                acc = psum.tile([P, c1 - c0], F32, name="acc", tag="bank%d" % (len(done) % BANKS))
+                done.append(u)
                 nc.tensor.matmul_mx(
                     out=acc[:],
                     lhsT=w2_codes[:, u * P : (u + 1) * P].bitcast(FP8X4),

@@ -65,17 +65,17 @@ def tile_picked_haarinp_none_p_kernel(tc, x_words, x_scales, w1, w2, offs, la, l
         nc.sync.dma_start(out=w2_raw[:], in_=w2.rearrange("(p j) c -> p j c", j=PACK))
 
         w1_grouped = keep.tile([P, PACK * H], BF16, name="w1_grouped", align_bytes=64)
-        dst = w1_grouped[:].rearrange("p (a b m j) -> p a m j b", a=2, b=2, j=PACK)
-        src = w1_raw[:].rearrange("p j (m b a) -> p a m j b", a=2, b=2)
-        nc.vector.tensor_copy(out=dst[:, 1], in_=src[:, 1])
-        nc.scalar.copy(out=dst[:, 0], in_=src[:, 0])
+        dst = w1_grouped[:].rearrange("p (h e m j) -> p h m j e", h=2, e=2, j=PACK)
+        src = w1_raw[:].rearrange("p j (m h e) -> p h m j e", h=2, e=2)
+        nc.vector.tensor_copy(out=dst[:, 0], in_=src[:, 0])
+        nc.scalar.copy(out=dst[:, 1], in_=src[:, 1])
 
         x_codes = keep.tile([P, S], U32, name="x_codes", align_bytes=64)
         w1_codes = [keep.tile([P, P], U32, name="w1_codes%d" % n, align_bytes=64) for n in range(PACK)]
         w1_sc = [keep.tile([P, P], U8, name="w1_sc%d" % n, align_bytes=64) for n in range(PACK)]
 
         def quantize_w1(n):
-            at = (SLOT[n] % 2 * 2 + SLOT[n] // 2) * H
+            at = SLOT[n] * H
             nc.vector.quantize_mx(out=w1_codes[n][:].bitcast(FP8X4), scales=w1_sc[n][:], in_=w1_grouped[:, at : at + H])
 
         def pick_words(c0, c1):
@@ -135,27 +135,28 @@ def tile_picked_haarinp_none_p_kernel(tc, x_words, x_scales, w1, w2, offs, la, l
             nc.scalar.copy(out=dst2[:, u * 32 : (u + 1) * 32], in_=src2[:, u * 32 : (u + 1) * 32])
 
         quantize_w1(0)
-        quantize_w1(1)
+        quantize_w1(2)
         pick_words(0, HALF)
         pick_words(HALF, HALF + P)
         pick_words(HALF + P, S)
-        quantize_w1(2)
+        quantize_w1(1)
         quantize_w1(3)
         first_product("scalar", 0, 0, HALF, 0)
         first_product("vector", 0, HALF, HALF + P, 1)
         first_product("scalar", 0, HALF + P, S, 2)
+        first_product("vector", 1, 0, P, 3)
+        first_product("scalar", 1, P, HALF, 4)
         fetch(0)
-        first_product("vector", 1, 0, HALF, 0)
+        first_product("vector", 1, HALF, S, 1)
         put_sum(0)
-        first_product("scalar", 1, HALF, S, 1)
-        first_product("scalar", 2, 0, HALF, 2)
+        first_product("scalar", 2, 0, HALF, 4)
         fetch(1)
         put_sum(1)
         negate_pair(0)
         put_diff(0)
         put_diff(1)
-        first_product("scalar", 2, HALF, S, 0)
-        first_product("scalar", 3, 0, S, 1)
+        first_product("scalar", 2, HALF, S, 1)
+        first_product("scalar", 3, 0, S, 4)
         fetch(2)
         fetch(3)
         join(0)

@@ -176,9 +176,9 @@ def tile_picked_haarinp_none_p_kernel(tc, x_words, x_scales, w1, w2, offs, la, l
         nc.scalar.copy(out=first_gain[:], in_=gain[:])
 
         def round_z(engine, n, c0, c1, scale):
-            src_z = pair[n][:].rearrange("p (h c) -> p c h", h=2)[:, c0:c1, :]
+            src_z = pair[n][:].rearrange("p (h c i) -> p c h i", h=2, i=4)[:, c0 // 4 : c1 // 4]
             at = max(c for c in z_grouped if c <= c0)
-            dst_z = z_grouped[at][:, c0 - at : c1 - at, 2 * n : 2 * n + 2]
+            dst_z = z_grouped[at][:, c0 - at : c1 - at, 2 * n : 2 * n + 2].rearrange("p (c i) t -> p c t i", i=4)
             if engine == "scalar":
                 nc.scalar.activation(out=dst_z, in_=src_z, func=COPY, scale=scale)
             else:

@@ -14,6 +14,7 @@ U8 = mybir.dt.uint8
 FP8X4 = mybir.dt.float8_e4m3fn_x4
 COPY = mybir.ActivationFunctionType.Copy
 ADD = mybir.AluOpType.add
+SUB = mybir.AluOpType.subtract
 MULT = mybir.AluOpType.mult
 
 P = 128
@@ -22,7 +23,7 @@ HALF = S // 2
 GAIN = 0.75
 BANKS = 8
 SLOT = (1, 3, 0, 2)
-CHUNKS = ((0, P), (P, HALF), (HALF, S))
+CHUNKS = tuple((c, c + P) for c in range(0, S, P))
 
 
 def tile_picked_haarinp_none_p_kernel(tc, x_words, x_scales, w1, w2, offs, la, lb, out):
@@ -45,8 +46,8 @@ def tile_picked_haarinp_none_p_kernel(tc, x_words, x_scales, w1, w2, offs, la, l
         nc.vector.memset(x_sc[:].bitcast(I32), 0)
         one = keep.tile([P, 1], F32, name="one")
         nc.vector.memset(one[:], 1.0)
-        minus = keep.tile([P, 1], F32, name="minus")
-        nc.scalar.activation(out=minus[:], in_=one[:], func=COPY, scale=-1.0)
+        gain = keep.tile([P, 1], F32, name="gain")
+        nc.scalar.activation(out=gain[:], in_=one[:], func=COPY, scale=GAIN)
 
         w1_rows = w1.rearrange("(p j) c -> p j c", j=PACK)
         nc.sync.dma_start(out=w1_raw[:, :2], in_=w1_rows[:, :2])
@@ -103,36 +104,93 @@ def tile_picked_haarinp_none_p_kernel(tc, x_words, x_scales, w1, w2, offs, la, l
         pair = [keep.tile([P, 2 * S], F32, name="pair%d" % n) for n in range(2)]
         window = early + pair
         z_grouped = {c0: keep.tile([P, c1 - c0, PACK], BF16, name="z_grouped%d" % c0, align_bytes=64) for c0, c1 in CHUNKS}
-        a = [keep.tile([P, V], F32, name="a%d" % n, tag="a%d" % n, align_bytes=64) for n in range(PACK)]
-        b = keep.tile([P, PACK, V], F32, name="b")
-        nb = {}
+        first_a = keep.tile([P, V], F32, name="first_a")
+        b = [keep.tile([P, V], F32, name="b%d" % n, tag="b%d" % n, align_bytes=64) for n in range(PACK)]
+        sm = [keep.tile([P, V], F32, name="sm%d" % n, tag="sm%d" % n, align_bytes=64) for n in range(PACK)]
+        df = {}
 
-        def fetch(n):
-            nc.scalar.activation(out=b[:, n, :], in_=y[n][:].indirect(lb_sb[:]), func=COPY)
-            if n == 0:
-                nc.vector.tensor_copy(out=a[n][:], in_=y[n][:].indirect(la_sb[:]))
-            else:
-                nc.scalar.activation(out=a[n][:], in_=y[n][:].indirect(la_sb[:]), func=COPY)
+        def fetch_b(n):
+            nc.scalar.activation(out=b[n][:], in_=y[n][:].indirect(lb_sb[:]), func=COPY)
 
-        def negate_pair(n):
-            nb[n] = keep.tile([P, 2, V], F32, name="nb", tag="y%d" % (n + 1), align_bytes=64)
-            nc.scalar.activation(out=nb[n][:], in_=b[:, n : n + 2, :], func=COPY, scale=minus[:])
+        def make_sum(n):
+            nc.vector.tensor_tensor(sm[n][:], y[n][:].indirect(la_sb[:]), b[n][:], ADD)
+
+        def make_diff(n, tag):
+            df[n] = keep.tile([P, V], F32, name="df%d" % n, tag=tag, align_bytes=64)
+            nc.vector.scalar_tensor_tensor(out=df[n][:], in0=b[n][:], scalar=-2.0, in1=sm[n][:], op0=MULT, op1=ADD)
 
         def put_sum(n):
-            nc.vector.tensor_tensor(window[n][:].indirect(la_sb[:]), a[n][:], b[:, n, :], ADD)
+            nc.vector.tensor_copy(window[n][:].indirect(la_sb[:]), sm[n][:])
 
         def put_diff(n):
-            nc.vector.tensor_tensor(window[n][:].indirect(lb_sb[:]), a[n][:], nb[n - n % 2][:, n % 2, :], ADD)
+            nc.scalar.activation(out=window[n][:].indirect(lb_sb[:]), in_=df[n][:], func=COPY)
 
-        def join(n):
-            nc.scalar.copy(out=pair[n][:, S:], in_=early[n][:])
+        def join(engine, n):
+            if engine == "scalar":
+                nc.scalar.copy(out=pair[n][:, S:], in_=early[n][:])
+            else:
+                nc.vector.tensor_copy(out=pair[n][:, S:], in_=early[n][:])
 
-        w2_grouped = keep.tile([P, N * PACK], BF16, name="w2_grouped", align_bytes=64)
-        dst2 = w2_grouped[:].rearrange("p (c i j) -> p c j i", i=4, j=PACK)
-        src2 = w2_raw[:].rearrange("p j (c i) -> p c j i", i=4)
+        w2_grouped = {}
+        src2 = w2_raw[:].rearrange("p j c -> p c j")
 
-        def round_w2(u):
-            nc.scalar.copy(out=dst2[:, u * 32 : (u + 1) * 32], in_=src2[:, u * 32 : (u + 1) * 32])
+        def round_w2(half, tag):
+            w2_grouped[half] = keep.tile([P, N // 2, PACK], BF16, name="w2_grouped", tag=tag, align_bytes=64)
+            nc.gpsimd.tensor_scalar(out=w2_grouped[half][:], in0=src2[:, half * N // 2 : (half + 1) * N // 2], scalar1=1.0, scalar2=0.0, op0=MULT, op1=ADD)
+
+        def round_z(engine, n, c0, c1):
+            src_z = pair[n][:].rearrange("p (h c i) -> p c h i", h=2, i=4)[:, c0 // 4 : c1 // 4]
+            at = max(c for c in z_grouped if c <= c0)
+            dst_z = z_grouped[at][:, c0 - at : c1 - at, 2 * n : 2 * n + 2].rearrange("p (c i) t -> p c t i", i=4)
+            if engine == "scalar":
+                nc.scalar.activation(out=dst_z, in_=src_z, func=COPY, scale=gain[:])
+            else:
+                nc.vector.tensor_scalar(out=dst_z, in0=src_z, scalar1=GAIN, scalar2=None, op0=MULT)
+
+        w2_codes = keep.tile([P, N], U32, name="w2_codes", align_bytes=64)
+        w2_sc = {}
+        z_codes = keep.tile([P, S], U32, name="z_codes", align_bytes=64)
+        z_sc = keep.tile([P, S], U8, name="z_sc", align_bytes=64)
+
+        def quantize_w2(half, tag):
+            m0, m1 = half * N // 2, (half + 1) * N // 2
+            w2_sc[half] = keep.tile([P, N // 2], U8, name="w2_sc", tag=tag, align_bytes=64)
+            nc.vector.quantize_mx(
+                out=w2_codes[:, m0:m1].bitcast(FP8X4),
+                scales=w2_sc[half][:],
+                in_=w2_grouped[half][:].rearrange("p c j -> p (c j)"),
+            )
+
+        def quantize_z(c0, c1):
+            nc.vector.quantize_mx(
+                out=z_codes[:, c0:c1].bitcast(FP8X4),
+                scales=z_sc[:, c0:c1],
+                in_=z_grouped[c0][:].rearrange("p c t -> p (c t)"),
+            )
+
+        out_blocks = out.rearrange("(u p) c -> p u c", p=P)
+
+        done = []
+
+        def second_product(engine, u0, u1, c0, c1):
+            acc = psum.tile([P, u1 - u0, c1 - c0], F32, name="acc", tag="bank%d" % (len(done) % BANKS))
+            done.append(u0)
+            for u in range(u0, u1):
+                nc.tensor.matmul_mx(
+                    out=acc[:, u - u0, :],
+                    lhsT=w2_codes[:, u * P : (u + 1) * P].bitcast(FP8X4),
+                    lhsT_scale=w2_sc[u // 2][:, u % 2 * P : (u % 2 + 1) * P],
+                    rhs=z_codes[:, c0:c1].bitcast(FP8X4),
+                    rhs_scale=z_sc[:, c0:c1],
+                    start=True,
+                    stop=True,
+                )
+            res = keep.tile([P, u1 - u0, c1 - c0], F32, name="res%d_%d" % (u0, c0))
+            if engine == "scalar":
+                nc.scalar.copy(out=res[:], in_=acc[:])
+            else:
+                nc.vector.tensor_copy(out=res[:], in_=acc[:])
+            nc.sync.dma_start(out=out_blocks[:, u0:u1, c0:c1], in_=res[:])
 
         quantize_w1(0)
         quantize_w1(2)
@@ -146,105 +204,56 @@ def tile_picked_haarinp_none_p_kernel(tc, x_words, x_scales, w1, w2, offs, la, l
         first_product("scalar", 0, HALF + P, S, 2)
         first_product("vector", 1, 0, P, 3)
         first_product("scalar", 1, P, HALF, 4)
-        fetch(0)
-        first_product("vector", 1, HALF, S, 1)
-        put_sum(0)
-        first_product("scalar", 2, 0, HALF, 4)
-        fetch(1)
-        put_sum(1)
-        negate_pair(0)
-        put_diff(0)
-        put_diff(1)
-        first_product("scalar", 2, HALF, S, 1)
+        fetch_b(0)
+        nc.vector.tensor_copy(out=first_a[:], in_=y[0][:].indirect(la_sb[:]))
+        first_product("scalar", 1, HALF, S, 1)
+        nc.vector.tensor_tensor(window[0][:].indirect(la_sb[:]), first_a[:], b[0][:], ADD)
+        df[0] = keep.tile([P, V], F32, name="df0")
+        nc.vector.tensor_tensor(df[0][:], first_a[:], b[0][:], SUB)
+        fetch_b(1)
         first_product("scalar", 3, 0, S, 4)
-        fetch(2)
-        fetch(3)
-        join(0)
-        put_sum(2)
-        round_w2(0)
-        join(1)
-        put_sum(3)
-        negate_pair(2)
-        put_diff(2)
+        fetch_b(3)
+        first_product("scalar", 2, 0, S, 1)
+        fetch_b(2)
+        make_sum(1)
+        put_diff(0)
+        make_diff(1, "df1")
+        put_sum(1)
+        round_w2(0, "b1")
+        put_diff(1)
+        make_sum(3)
+        make_sum(2)
+        join("vector", 0)
+        make_diff(3, "y2")
+        make_diff(2, "df2")
+        round_w2(1, "b2")
         put_diff(3)
-        for u in range(1, PACK):
-            round_w2(u)
+        put_sum(2)
+        quantize_w2(0, "b3")
+        join("vector", 1)
+        put_sum(3)
+        put_diff(2)
 
-        gain = keep.tile([P, 1], F32, name="gain", tag="w2_raw", align_bytes=64)
-        nc.scalar.activation(out=gain[:], in_=one[:], func=COPY, scale=GAIN)
-        first_gain = keep.tile([P, 1], F32, name="first_gain", tag="first_gain", align_bytes=64)
-        nc.scalar.copy(out=first_gain[:], in_=gain[:])
-
-        def round_z(engine, n, c0, c1, scale):
-            src_z = pair[n][:].rearrange("p (h c i) -> p c h i", h=2, i=4)[:, c0 // 4 : c1 // 4]
-            at = max(c for c in z_grouped if c <= c0)
-            dst_z = z_grouped[at][:, c0 - at : c1 - at, 2 * n : 2 * n + 2].rearrange("p (c i) t -> p c t i", i=4)
-            if engine == "scalar":
-                nc.scalar.activation(out=dst_z, in_=src_z, func=COPY, scale=scale)
-            else:
-                nc.vector.tensor_scalar(out=dst_z, in0=src_z, scalar1=scale, scalar2=None, op0=MULT)
-
-        w2_codes = keep.tile([P, N], U32, name="w2_codes", align_bytes=64)
-        w2_sc = {}
-        z_codes = keep.tile([P, S], U32, name="z_codes", align_bytes=64)
-        z_sc = keep.tile([P, S], U8, name="z_sc", align_bytes=64)
-
-        def quantize_w2(half, tag):
-            m0, m1 = half * N // 2, (half + 1) * N // 2
-            w2_sc[half] = keep.tile([P, N // 2], U8, name="w2_sc", tag=tag, align_bytes=64)
-            nc.vector.quantize_mx(out=w2_codes[:, m0:m1].bitcast(FP8X4), scales=w2_sc[half][:], in_=w2_grouped[:, PACK * m0 : PACK * m1])
-
-        def quantize_z(c0, c1):
-            nc.vector.quantize_mx(
-                out=z_codes[:, c0:c1].bitcast(FP8X4),
-                scales=z_sc[:, c0:c1],
-                in_=z_grouped[c0][:].rearrange("p c t -> p (c t)"),
-            )
-
-        out_blocks = out.rearrange("(u p) c -> p u c", p=P)
-
-        done = []
-
-        def second_product(pieces):
-            u0, u1 = pieces[0][1], pieces[-1][1] + 1
-            s0, s1 = pieces[0][2], pieces[-1][3]
-            res = keep.tile([P, u1 - u0, s1 - s0], F32, name="res%d_%d" % (u0, s0))
-            for engine, u, c0, c1 in pieces:
-                acc = psum.tile([P, c1 - c0], F32, name="acc", tag="bank%d" % (len(done) % BANKS))
-                done.append(u)
-                nc.tensor.matmul_mx(
-                    out=acc[:],
-                    lhsT=w2_codes[:, u * P : (u + 1) * P].bitcast(FP8X4),
-                    lhsT_scale=w2_sc[u // 2][:, u % 2 * P : (u % 2 + 1) * P],
-                    rhs=z_codes[:, c0:c1].bitcast(FP8X4),
-                    rhs_scale=z_sc[:, c0:c1],
-                    start=True,
-                    stop=True,
-                )
-                if engine == "scalar":
-                    nc.scalar.copy(out=res[:, u - u0, c0 - s0 : c1 - s0], in_=acc[:])
-                else:
-                    nc.vector.tensor_copy(out=res[:, u - u0, c0 - s0 : c1 - s0], in_=acc[:])
-            nc.sync.dma_start(out=out_blocks[:, u0:u1, s0:s1], in_=res[:])
-
-        round_z("scalar", 0, 0, P, gain[:])
-        round_z("scalar", 0, HALF, S, gain[:])
-        quantize_w2(0, "a3")
-        round_z("scalar", 1, 0, P, first_gain[:])
-        round_z("scalar", 0, P, HALF, gain[:])
-        round_z("vector", 1, P, HALF, gain[:])
-        round_z("vector", 1, HALF, 3 * P, gain[:])
-        round_z("scalar", 1, 3 * P, S, gain[:])
+        round_z("scalar", 0, 0, P)
+        round_z("vector", 1, 0, P)
+        round_z("scalar", 0, P, HALF)
+        round_z("vector", 1, P, HALF)
         quantize_z(0, P)
-        quantize_w2(1, "first_gain")
         quantize_z(P, HALF)
-        quantize_z(HALF, S)
-        second_product([("scalar", 0, 0, P)])
-        second_product([("scalar", 1, 0, P)])
-        second_product([("scalar", 2, 0, P), ("vector", 3, 0, P)])
-        second_product([("scalar", 0, P, HALF), ("vector", 1, P, HALF)])
-        second_product([("scalar", 2, P, HALF), ("vector", 3, P, HALF)])
-        second_product([("scalar", 0, HALF, S)])
-        second_product([("vector", 1, HALF, S)])
-        second_product([("scalar", 2, HALF, S)])
-        second_product([("vector", 3, HALF, 3 * P), ("scalar", 3, 3 * P, S)])
+        quantize_w2(1, "sm3")
+        round_z("scalar", 0, HALF, 3 * P)
+        round_z("vector", 1, HALF, 3 * P)
+        round_z("scalar", 0, 3 * P, S)
+        round_z("vector", 1, 3 * P, S)
+        quantize_z(HALF, 3 * P)
+        quantize_z(3 * P, S)
+        second_product("scalar", 0, 1, 0, P)
+        second_product("scalar", 1, 2, 0, P)
+        second_product("scalar", 0, 2, P, HALF)
+        second_product("scalar", 2, 4, 0, P)
+        second_product("vector", 2, 4, P, HALF)
+        second_product("scalar", 0, 1, HALF, S)
+        second_product("vector", 1, 2, HALF, S)
+        second_product("scalar", 2, 3, HALF, S)
+        second_product("vector", 3, 4, HALF, 3 * P)
+        second_product("scalar", 3, 4, 3 * P, S)

@@ -104,39 +104,38 @@ def tile_picked_haarinp_none_p_kernel(tc, x_words, x_scales, w1, w2, offs, la, l
         pair = [keep.tile([P, 2 * S], F32, name="pair%d" % n) for n in range(2)]
         window = early + pair
         z_grouped = {c0: keep.tile([P, c1 - c0, PACK], BF16, name="z_grouped%d" % c0, align_bytes=64) for c0, c1 in CHUNKS}
-        first_a = keep.tile([P, V], F32, name="first_a")
+        a = [keep.tile([P, V], F32, name="a%d" % n, tag="a%d" % n, align_bytes=64) for n in range(PACK)]
         b = [keep.tile([P, V], F32, name="b%d" % n, tag="b%d" % n, align_bytes=64) for n in range(PACK)]
-        sm = [keep.tile([P, V], F32, name="sm%d" % n, tag="sm%d" % n, align_bytes=64) for n in range(PACK)]
-        df = {}
+        df = [keep.tile([P, V], F32, name="df%d" % n, tag="df%d" % n, align_bytes=64) for n in range(PACK)]
 
-        def fetch_b(n):
+        def fetch(n):
             nc.scalar.activation(out=b[n][:], in_=y[n][:].indirect(lb_sb[:]), func=COPY)
+            if n == 0:
+                nc.vector.tensor_copy(out=a[n][:], in_=y[n][:].indirect(la_sb[:]))
+            else:
+                nc.scalar.activation(out=a[n][:], in_=y[n][:].indirect(la_sb[:]), func=COPY)
 
-        def make_sum(n):
-            nc.vector.tensor_tensor(sm[n][:], y[n][:].indirect(la_sb[:]), b[n][:], ADD)
-
-        def make_diff(n, tag):
-            df[n] = keep.tile([P, V], F32, name="df%d" % n, tag=tag, align_bytes=64)
-            nc.vector.scalar_tensor_tensor(out=df[n][:], in0=b[n][:], scalar=-2.0, in1=sm[n][:], op0=MULT, op1=ADD)
+        def make_diff(n):
+            nc.vector.tensor_tensor(df[n][:], a[n][:], b[n][:], SUB)
 
         def put_sum(n):
-            nc.vector.tensor_copy(window[n][:].indirect(la_sb[:]), sm[n][:])
+            nc.vector.tensor_tensor(window[n][:].indirect(la_sb[:]), a[n][:], b[n][:], ADD)
 
         def put_diff(n):
             nc.scalar.activation(out=window[n][:].indirect(lb_sb[:]), in_=df[n][:], func=COPY)
 
-        def join(engine, n):
-            if engine == "scalar":
-                nc.scalar.copy(out=pair[n][:, S:], in_=early[n][:])
-            else:
-                nc.vector.tensor_copy(out=pair[n][:, S:], in_=early[n][:])
+        def join(n):
+            nc.vector.tensor_copy(out=pair[n][:, S:], in_=early[n][:])
 
         w2_grouped = {}
-        src2 = w2_raw[:].rearrange("p j c -> p c j")
+        src2 = w2_raw[:].rearrange("p j (c i) -> p c j i", i=4)
 
         def round_w2(half, tag):
             w2_grouped[half] = keep.tile([P, N // 2, PACK], BF16, name="w2_grouped", tag=tag, align_bytes=64)
-            nc.gpsimd.tensor_scalar(out=w2_grouped[half][:], in0=src2[:, half * N // 2 : (half + 1) * N // 2], scalar1=1.0, scalar2=0.0, op0=MULT, op1=ADD)
+            nc.vector.tensor_copy(
+                out=w2_grouped[half][:].rearrange("p (c i) j -> p c j i", i=4),
+                in_=src2[:, half * N // 8 : (half + 1) * N // 8],
+            )
 
         def round_z(engine, n, c0, c1):
             src_z = pair[n][:].rearrange("p (h c i) -> p c h i", h=2, i=4)[:, c0 // 4 : c1 // 4]
@@ -204,43 +203,38 @@ def tile_picked_haarinp_none_p_kernel(tc, x_words, x_scales, w1, w2, offs, la, l
         first_product("scalar", 0, HALF + P, S, 2)
         first_product("vector", 1, 0, P, 3)
         first_product("scalar", 1, P, HALF, 4)
-        fetch_b(0)
-        nc.vector.tensor_copy(out=first_a[:], in_=y[0][:].indirect(la_sb[:]))
-        first_product("scalar", 1, HALF, S, 1)
-        nc.vector.tensor_tensor(window[0][:].indirect(la_sb[:]), first_a[:], b[0][:], ADD)
-        df[0] = keep.tile([P, V], F32, name="df0")
-        nc.vector.tensor_tensor(df[0][:], first_a[:], b[0][:], SUB)
-        fetch_b(1)
-        first_product("scalar", 3, 0, S, 4)
-        fetch_b(3)
-        first_product("scalar", 2, 0, S, 1)
-        fetch_b(2)
-        make_sum(1)
+        fetch(0)
+        first_product("vector", 1, HALF, S, 6)
+        put_sum(0)
+        make_diff(0)
+        first_product("scalar", 3, 0, S, 5)
+        fetch(1)
+        first_product("vector", 2, 0, S, 6)
+        fetch(3)
         put_diff(0)
-        make_diff(1, "df1")
+        fetch(2)
         put_sum(1)
-        round_w2(0, "b1")
-        put_diff(1)
-        make_sum(3)
-        make_sum(2)
-        join("vector", 0)
-        make_diff(3, "y2")
-        make_diff(2, "df2")
-        round_w2(1, "b2")
-        put_diff(3)
-        put_sum(2)
-        quantize_w2(0, "b3")
-        join("vector", 1)
+        make_diff(1)
         put_sum(3)
+        make_diff(3)
+        join(0)
+        make_diff(2)
+        put_sum(2)
+        put_diff(1)
+        put_diff(3)
         put_diff(2)
+        round_w2(0, "y2")
+        round_w2(1, "a2")
+        join(1)
 
-        round_z("scalar", 0, 0, P)
+        quantize_w2(0, "w2_sc0")
         round_z("vector", 1, 0, P)
-        round_z("scalar", 0, P, HALF)
+        round_z("vector", 0, 0, P)
         round_z("vector", 1, P, HALF)
+        round_z("scalar", 0, P, HALF)
         quantize_z(0, P)
         quantize_z(P, HALF)
-        quantize_w2(1, "sm3")
+        quantize_w2(1, "df2")
         round_z("scalar", 0, HALF, 3 * P)
         round_z("vector", 1, HALF, 3 * P)
         round_z("scalar", 0, 3 * P, S)
@@ -250,8 +244,8 @@ def tile_picked_haarinp_none_p_kernel(tc, x_words, x_scales, w1, w2, offs, la, l
         second_product("scalar", 0, 1, 0, P)
         second_product("scalar", 1, 2, 0, P)
         second_product("scalar", 0, 2, P, HALF)
-        second_product("scalar", 2, 4, 0, P)
-        second_product("vector", 2, 4, P, HALF)
+        second_product("scalar", 2, 3, 0, HALF)
+        second_product("vector", 3, 4, 0, HALF)
         second_product("scalar", 0, 1, HALF, S)
         second_product("vector", 1, 2, HALF, S)
         second_product("scalar", 2, 3, HALF, S)

@@ -167,16 +167,16 @@ def tile_picked_haarinp_none_p_kernel(tc, x_words, x_scales, w1, w2, offs, la, l
                 in_=z_grouped[c0][:].rearrange("p c t -> p (c t)"),
             )
 
-        out_blocks = out.rearrange("(u p) c -> p u c", p=P)
-
         done = []
 
-        def second_product(engine, u0, u1, c0, c1):
-            acc = psum.tile([P, u1 - u0, c1 - c0], F32, name="acc", tag="bank%d" % (len(done) % BANKS))
-            done.append(u0)
-            for u in range(u0, u1):
+        def second_product(u, pieces):
+            s0, s1 = pieces[0][1], pieces[-1][2]
+            res = keep.tile([P, s1 - s0], F32, name="res%d_%d" % (u, s0))
+            for engine, c0, c1 in pieces:
+                acc = psum.tile([P, c1 - c0], F32, name="acc", tag="bank%d" % (len(done) % BANKS))
+                done.append(u)
                 nc.tensor.matmul_mx(
-                    out=acc[:, u - u0, :],
+                    out=acc[:],
                     lhsT=w2_codes[:, u * P : (u + 1) * P].bitcast(FP8X4),
                     lhsT_scale=w2_sc[u // 2][:, u % 2 * P : (u % 2 + 1) * P],
                     rhs=z_codes[:, c0:c1].bitcast(FP8X4),
@@ -184,12 +184,11 @@ def tile_picked_haarinp_none_p_kernel(tc, x_words, x_scales, w1, w2, offs, la, l
                     start=True,
                     stop=True,
                 )
-            res = keep.tile([P, u1 - u0, c1 - c0], F32, name="res%d_%d" % (u0, c0))
-            if engine == "scalar":
-                nc.scalar.copy(out=res[:], in_=acc[:])
-            else:
-                nc.vector.tensor_copy(out=res[:], in_=acc[:])
-            nc.sync.dma_start(out=out_blocks[:, u0:u1, c0:c1], in_=res[:])
+                if engine == "scalar":
+                    nc.scalar.copy(out=res[:, c0 - s0 : c1 - s0], in_=acc[:])
+                else:
+                    nc.vector.tensor_copy(out=res[:, c0 - s0 : c1 - s0], in_=acc[:])
+            nc.sync.dma_start(out=out[u * P : (u + 1) * P, s0:s1], in_=res[:])
 
         quantize_w1(0)
         quantize_w1(2)
@@ -241,13 +240,11 @@ def tile_picked_haarinp_none_p_kernel(tc, x_words, x_scales, w1, w2, offs, la, l
         round_z("vector", 1, 3 * P, S)
         quantize_z(HALF, 3 * P)
         quantize_z(3 * P, S)
-        second_product("scalar", 0, 1, 0, P)
-        second_product("scalar", 1, 2, 0, P)
-        second_product("scalar", 0, 2, P, HALF)
-        second_product("scalar", 2, 3, 0, HALF)
-        second_product("vector", 3, 4, 0, HALF)
-        second_product("scalar", 0, 1, HALF, S)
-        second_product("vector", 1, 2, HALF, S)
-        second_product("scalar", 2, 3, HALF, S)
-        second_product("vector", 3, 4, HALF, 3 * P)
-        second_product("scalar", 3, 4, 3 * P, S)
+        second_product(0, [("scalar", 0, P), ("scalar", P, HALF)])
+        second_product(1, [("scalar", 0, HALF)])
+        second_product(2, [("vector", 0, HALF)])
+        second_product(3, [("scalar", 0, HALF)])
+        second_product(0, [("vector", HALF, S)])
+        second_product(1, [("scalar", HALF, S)])
+        second_product(2, [("vector", HALF, S)])
+        second_product(3, [("scalar", HALF, 3 * P), ("vector", 3 * P, S)])

@@ -23,7 +23,7 @@ HALF = S // 2
 GAIN = 0.75
 BANKS = 8
 SLOT = (1, 3, 0, 2)
-CHUNKS = tuple((c, c + P) for c in range(0, S, P))
+CHUNKS = ((0, P), (P, HALF), (HALF, S))
 
 
 def tile_picked_haarinp_none_p_kernel(tc, x_words, x_scales, w1, w2, offs, la, lb, out):
@@ -95,100 +95,103 @@ def tile_picked_haarinp_none_p_kernel(tc, x_words, x_scales, w1, w2, offs, la, l
                 start=True,
                 stop=True,
             )
-            if engine == "scalar":
+            if n == 3:
+                nc.scalar.activation(out=y[n][:, c0:c1], in_=acc[:], func=COPY, scale=gain[:])
+            elif engine == "scalar":
                 nc.scalar.copy(out=y[n][:, c0:c1], in_=acc[:])
             else:
                 nc.vector.tensor_copy(out=y[n][:, c0:c1], in_=acc[:])
 
-        early = [keep.tile([P, S], F32, name="early%d" % n) for n in range(2)]
+        early = [keep.tile([P, S], F32, name="early%d" % n, tag="early%d" % n, align_bytes=64) for n in range(2)]
         pair = [keep.tile([P, 2 * S], F32, name="pair%d" % n) for n in range(2)]
         window = early + pair
-        z_grouped = {c0: keep.tile([P, c1 - c0, PACK], BF16, name="z_grouped%d" % c0, align_bytes=64) for c0, c1 in CHUNKS}
-        a = [keep.tile([P, V], F32, name="a%d" % n, tag="a%d" % n, align_bytes=64) for n in range(PACK)]
+        a = {n: keep.tile([P, V], F32, name="a%d" % n, tag="a%d" % n, align_bytes=64) for n in (0, 1, 3)}
         b = [keep.tile([P, V], F32, name="b%d" % n, tag="b%d" % n, align_bytes=64) for n in range(PACK)]
-        df = [keep.tile([P, V], F32, name="df%d" % n, tag="df%d" % n, align_bytes=64) for n in range(PACK)]
+        df = {0: keep.tile([P, V], F32, name="df0")}
+
+        sm = [None] + [keep.tile([P, V], F32, name="sm%d" % n, tag="sm%d" % n, align_bytes=64) for n in range(1, PACK)]
 
         def fetch(n):
             nc.scalar.activation(out=b[n][:], in_=y[n][:].indirect(lb_sb[:]), func=COPY)
             if n == 0:
                 nc.vector.tensor_copy(out=a[n][:], in_=y[n][:].indirect(la_sb[:]))
-            else:
+            elif n != 2:
                 nc.scalar.activation(out=a[n][:], in_=y[n][:].indirect(la_sb[:]), func=COPY)
 
-        def make_diff(n):
-            nc.vector.tensor_tensor(df[n][:], a[n][:], b[n][:], SUB)
+        def make_sum(n):
+            nc.gpsimd.tensor_tensor(sm[n][:], a[n][:], b[n][:], ADD)
+
+        def make_diff(n, tag):
+            df[n] = keep.tile([P, V], F32, name="df%d" % n, tag=tag, align_bytes=64)
+            nc.gpsimd.tensor_tensor(df[n][:], a[n][:], b[n][:], SUB)
 
         def put_sum(n):
-            nc.vector.tensor_tensor(window[n][:].indirect(la_sb[:]), a[n][:], b[n][:], ADD)
+            nc.vector.tensor_copy(window[n][:].indirect(la_sb[:]), sm[n][:])
 
         def put_diff(n):
             nc.scalar.activation(out=window[n][:].indirect(lb_sb[:]), in_=df[n][:], func=COPY)
 
         def join(n):
-            nc.vector.tensor_copy(out=pair[n][:, S:], in_=early[n][:])
+            if n == 0:
+                nc.gpsimd.tensor_scalar(out=pair[n][:, S:], in0=early[n][:], scalar1=1.0, scalar2=0.0, op0=MULT, op1=ADD)
+            else:
+                nc.vector.tensor_scalar(out=pair[n][:, S:], in0=early[n][:], scalar1=late_gain[:], scalar2=None, op0=MULT)
 
-        w2_grouped = {}
         src2 = w2_raw[:].rearrange("p j (c i) -> p c j i", i=4)
-
-        def round_w2(half, tag):
-            w2_grouped[half] = keep.tile([P, N // 2, PACK], BF16, name="w2_grouped", tag=tag, align_bytes=64)
-            nc.vector.tensor_copy(
-                out=w2_grouped[half][:].rearrange("p (c i) j -> p c j i", i=4),
-                in_=src2[:, half * N // 8 : (half + 1) * N // 8],
-            )
 
         def round_z(engine, n, c0, c1):
             src_z = pair[n][:].rearrange("p (h c i) -> p c h i", h=2, i=4)[:, c0 // 4 : c1 // 4]
-            at = max(c for c in z_grouped if c <= c0)
+            at = max(c for c, end in CHUNKS if c <= c0)
             dst_z = z_grouped[at][:, c0 - at : c1 - at, 2 * n : 2 * n + 2].rearrange("p (c i) t -> p c t i", i=4)
             if engine == "scalar":
-                nc.scalar.activation(out=dst_z, in_=src_z, func=COPY, scale=gain[:])
+                nc.scalar.activation(out=dst_z, in_=src_z, func=COPY, scale=last_gain[:])
+            elif n == 1:
+                nc.vector.tensor_copy(out=dst_z, in_=src_z)
             else:
-                nc.vector.tensor_scalar(out=dst_z, in0=src_z, scalar1=GAIN, scalar2=None, op0=MULT)
+                nc.vector.tensor_scalar(out=dst_z, in0=src_z, scalar1=last_gain[:], scalar2=None, op0=MULT)
 
         w2_codes = keep.tile([P, N], U32, name="w2_codes", align_bytes=64)
         w2_sc = {}
         z_codes = keep.tile([P, S], U32, name="z_codes", align_bytes=64)
-        z_sc = keep.tile([P, S], U8, name="z_sc", align_bytes=64)
+        z_sc = {0: keep.tile([P, HALF], U8, name="z_sc", align_bytes=64)}
 
-        def quantize_w2(half, tag):
-            m0, m1 = half * N // 2, (half + 1) * N // 2
-            w2_sc[half] = keep.tile([P, N // 2], U8, name="w2_sc", tag=tag, align_bytes=64)
-            nc.vector.quantize_mx(
-                out=w2_codes[:, m0:m1].bitcast(FP8X4),
-                scales=w2_sc[half][:],
-                in_=w2_grouped[half][:].rearrange("p c j -> p (c j)"),
-            )
+        def quantize_w2(u0, u1, grouped, tag):
+            scales = keep.tile([P, (u1 - u0) * P], U8, name="w2_sc", tag=tag, align_bytes=64)
+            for u in range(u0, u1):
+                w2_sc[u] = scales[:, (u - u0) * P : (u - u0 + 1) * P]
+            nc.vector.quantize_mx(out=w2_codes[:, u0 * P : u1 * P].bitcast(FP8X4), scales=scales[:], in_=grouped.rearrange("p c j -> p (c j)"))
 
         def quantize_z(c0, c1):
             nc.vector.quantize_mx(
                 out=z_codes[:, c0:c1].bitcast(FP8X4),
-                scales=z_sc[:, c0:c1],
+                scales=z_sc[c0 // HALF][:, c0 % HALF : c0 % HALF + c1 - c0],
                 in_=z_grouped[c0][:].rearrange("p c t -> p (c t)"),
             )
 
         done = []
 
-        def second_product(u, pieces):
-            s0, s1 = pieces[0][1], pieces[-1][2]
-            res = keep.tile([P, s1 - s0], F32, name="res%d_%d" % (u, s0))
-            for engine, c0, c1 in pieces:
-                acc = psum.tile([P, c1 - c0], F32, name="acc", tag="bank%d" % (len(done) % BANKS))
-                done.append(u)
-                nc.tensor.matmul_mx(
-                    out=acc[:],
-                    lhsT=w2_codes[:, u * P : (u + 1) * P].bitcast(FP8X4),
-                    lhsT_scale=w2_sc[u // 2][:, u % 2 * P : (u % 2 + 1) * P],
-                    rhs=z_codes[:, c0:c1].bitcast(FP8X4),
-                    rhs_scale=z_sc[:, c0:c1],
-                    start=True,
-                    stop=True,
-                )
+        def second_product(pieces):
+            u0, u1 = pieces[0][1], pieces[-1][2]
+            s0, s1 = pieces[0][3], pieces[-1][4]
+            res = keep.tile([P, u1 - u0, s1 - s0], F32, name="res%d_%d" % (u0, s0))
+            for engine, v0, v1, c0, c1 in pieces:
+                acc = psum.tile([P, v1 - v0, c1 - c0], F32, name="acc", tag="bank%d" % (len(done) % BANKS))
+                done.append(v0)
+                for u in range(v0, v1):
+                    nc.tensor.matmul_mx(
+                        out=acc[:, u - v0, :],
+                        lhsT=w2_codes[:, u * P : (u + 1) * P].bitcast(FP8X4),
+                        lhsT_scale=w2_sc[u],
+                        rhs=z_codes[:, c0:c1].bitcast(FP8X4),
+                        rhs_scale=z_sc[c0 // HALF][:, c0 % HALF : c0 % HALF + c1 - c0],
+                        start=True,
+                        stop=True,
+                    )
                 if engine == "scalar":
-                    nc.scalar.copy(out=res[:, c0 - s0 : c1 - s0], in_=acc[:])
+                    nc.scalar.copy(out=res[:, v0 - u0 : v1 - u0, c0 - s0 : c1 - s0], in_=acc[:])
                 else:
-                    nc.vector.tensor_copy(out=res[:, c0 - s0 : c1 - s0], in_=acc[:])
-            nc.sync.dma_start(out=out[u * P : (u + 1) * P, s0:s1], in_=res[:])
+                    nc.vector.tensor_copy(out=res[:, v0 - u0 : v1 - u0, c0 - s0 : c1 - s0], in_=acc[:])
+            nc.sync.dma_start(out=out.rearrange("(u p) c -> p u c", p=P)[:, u0:u1, s0:s1], in_=res[:])
 
         quantize_w1(0)
         quantize_w1(2)
@@ -204,47 +207,59 @@ def tile_picked_haarinp_none_p_kernel(tc, x_words, x_scales, w1, w2, offs, la, l
         first_product("scalar", 1, P, HALF, 4)
         fetch(0)
         first_product("vector", 1, HALF, S, 6)
-        put_sum(0)
-        make_diff(0)
+        nc.vector.tensor_tensor(df[0][:], a[0][:], b[0][:], SUB)
+        nc.vector.tensor_tensor(window[0][:].indirect(la_sb[:]), a[0][:], b[0][:], ADD)
         first_product("scalar", 3, 0, S, 5)
         fetch(1)
         first_product("vector", 2, 0, S, 6)
         fetch(3)
         put_diff(0)
         fetch(2)
+        make_sum(1)
+        make_diff(1, "df1")
         put_sum(1)
-        make_diff(1)
-        put_sum(3)
-        make_diff(3)
+        a[2] = keep.tile([P, V], F32, name="a2", tag="a1", align_bytes=64)
+        nc.vector.tensor_copy(out=a[2][:], in_=y[2][:].indirect(la_sb[:]))
+        make_sum(3)
+        make_diff(3, "df3")
         join(0)
-        make_diff(2)
+        make_sum(2)
+        make_diff(2, "df2")
+        put_sum(3)
         put_sum(2)
         put_diff(1)
         put_diff(3)
         put_diff(2)
-        round_w2(0, "y2")
-        round_w2(1, "a2")
+        w2_last = keep.tile([P, P, PACK], BF16, name="w2_last", tag="a3", align_bytes=64)
+        nc.gpsimd.tensor_scalar(out=w2_last[:], in0=w2_raw[:].rearrange("p j c -> p c j")[:, 3 * P :], scalar1=1.0, scalar2=0.0, op0=MULT, op1=ADD)
+        late_gain = keep.tile([P, 1], F32, name="late_gain", tag="b2", align_bytes=64)
+        nc.vector.memset(late_gain[:], GAIN)
+        w2_first = keep.tile([P, 3 * P, PACK], BF16, name="w2_first", tag="a1", align_bytes=64)
+        nc.vector.tensor_copy(out=w2_first[:].rearrange("p (c i) j -> p c j i", i=4), in_=src2[:, : 3 * P // 4])
         join(1)
 
-        quantize_w2(0, "w2_sc0")
-        round_z("vector", 1, 0, P)
+        z_grouped = {
+            c0: keep.tile([P, c1 - c0, PACK], BF16, name="z_grouped%d" % c0, tag=tag, align_bytes=64)
+            for (c0, c1), tag in zip(CHUNKS, ("z_first", "z_second", "z_third"))
+        }
+        quantize_w2(0, 3, w2_first[:], "w2_sc0")
+        last_gain = keep.tile([P, 1], F32, name="last_gain", tag="early1", align_bytes=64)
+        nc.vector.memset(last_gain[:], GAIN)
+        for c0, c1 in CHUNKS:
+            round_z("vector", 1, c0, c1)
         round_z("vector", 0, 0, P)
-        round_z("vector", 1, P, HALF)
-        round_z("scalar", 0, P, HALF)
+        round_z("vector", 0, P, HALF)
+        round_z("scalar", 0, HALF, S)
         quantize_z(0, P)
         quantize_z(P, HALF)
-        quantize_w2(1, "df2")
-        round_z("scalar", 0, HALF, 3 * P)
-        round_z("vector", 1, HALF, 3 * P)
-        round_z("scalar", 0, 3 * P, S)
-        round_z("vector", 1, 3 * P, S)
-        quantize_z(HALF, 3 * P)
-        quantize_z(3 * P, S)
-        second_product(0, [("scalar", 0, P), ("scalar", P, HALF)])
-        second_product(1, [("scalar", 0, HALF)])
-        second_product(2, [("vector", 0, HALF)])
-        second_product(3, [("scalar", 0, HALF)])
-        second_product(0, [("vector", HALF, S)])
-        second_product(1, [("scalar", HALF, S)])
-        second_product(2, [("vector", HALF, S)])
-        second_product(3, [("scalar", HALF, 3 * P), ("vector", 3 * P, S)])
+        quantize_w2(3, 4, w2_last[:], "z_first")
+        z_sc[1] = keep.tile([P, HALF], U8, name="z_sc", tag="z_second", align_bytes=64)
+        quantize_z(HALF, S)
+        second_product([("scalar", 0, 2, 0, P)])
+        second_product([("scalar", 0, 2, P, HALF)])
+        second_product([("vector", 2, 3, 0, HALF)])
+        second_product([("scalar", 3, 4, 0, HALF)])
+        second_product([("vector", 0, 1, HALF, S)])
+        second_product([("scalar", 1, 2, HALF, S)])
+        second_product([("vector", 2, 3, HALF, S)])
+        second_product([("scalar", 3, 4, HALF, 3 * P), ("vector", 3, 4, 3 * P, S)])

@@ -255,11 +255,13 @@ def tile_picked_haarinp_none_p_kernel(tc, x_words, x_scales, w1, w2, offs, la, l
         quantize_w2(3, 4, w2_last[:], "z_first")
         z_sc[1] = keep.tile([P, HALF], U8, name="z_sc", tag="z_second", align_bytes=64)
         quantize_z(HALF, S)
-        second_product([("scalar", 0, 2, 0, P)])
+        second_product([("scalar", 0, 1, 0, P)])
+        second_product([("scalar", 1, 2, 0, P)])
         second_product([("scalar", 0, 2, P, HALF)])
         second_product([("vector", 2, 3, 0, HALF)])
         second_product([("scalar", 3, 4, 0, HALF)])
         second_product([("vector", 0, 1, HALF, S)])
         second_product([("scalar", 1, 2, HALF, S)])
         second_product([("vector", 2, 3, HALF, S)])
-        second_product([("scalar", 3, 4, HALF, 3 * P), ("vector", 3, 4, 3 * P, S)])
+        second_product([("scalar", 3, 4, HALF, 3 * P)])
+        second_product([("vector", 3, 4, 3 * P, S)])

@@ -61,7 +61,7 @@ def tile_picked_haarinp_none_p_kernel(tc, x_words, x_scales, w1, w2, offs, la, l
         s_picked = keep.tile([P, S], U8, name="s_picked", tag="w2_raw", align_bytes=64)
         nc.vector.tensor_copy(out=s_picked[:], in_=s_table[:].indirect(offs_sb[:]))
         for r in range(4):
-            nc.scalar.dma_start(out=x_sc[r:P:32, :].bitcast(I32), in_=s_picked[32 + 4 * r : 96 : 16, :].bitcast(I32))
+            nc.sync.dma_start(out=x_sc[r:P:32, :].bitcast(I32), in_=s_picked[32 + 4 * r : 96 : 16, :].bitcast(I32))
         w2_raw = keep.tile([P, PACK, N], F32, name="w2_raw", tag="w2_raw", align_bytes=64)
         nc.sync.dma_start(out=w2_raw[:], in_=w2.rearrange("(p j) c -> p j c", j=PACK))
 
@@ -193,13 +193,11 @@ def tile_picked_haarinp_none_p_kernel(tc, x_words, x_scales, w1, w2, offs, la, l
                     nc.vector.tensor_copy(out=res[:, v0 - u0 : v1 - u0, c0 - s0 : c1 - s0], in_=acc[:])
             nc.sync.dma_start(out=out.rearrange("(u p) c -> p u c", p=P)[:, u0:u1, s0:s1], in_=res[:])
 
-        quantize_w1(0)
-        quantize_w1(2)
+        for n in (0, 2, 1, 3):
+            quantize_w1(n)
         pick_words(0, HALF)
         pick_words(HALF, HALF + P)
         pick_words(HALF + P, S)
-        quantize_w1(1)
-        quantize_w1(3)
         first_product("scalar", 0, 0, HALF, 0)
         first_product("vector", 0, HALF, HALF + P, 1)
         first_product("scalar", 0, HALF + P, S, 2)

from contextlib import ExitStack

import concourse.mybir as mybir

K, T, S, V, N, H = 512, 2048, 512, 256, 512, 512
FLOPS = 2 * K * H * S + 2 * H * N * S

F32 = mybir.dt.float32
BF16 = mybir.dt.bfloat16
I32 = mybir.dt.int32
U32 = mybir.dt.uint32
U16 = mybir.dt.uint16
U8 = mybir.dt.uint8
FP8X4 = mybir.dt.float8_e4m3fn_x4
COPY = mybir.ActivationFunctionType.Copy
ADD = mybir.AluOpType.add
SUB = mybir.AluOpType.subtract
MULT = mybir.AluOpType.mult

P = 128
PACK = 4
HALF = S // 2
GAIN = 0.75
BANKS = 8
SLOT = (1, 3, 0, 2)
CHUNKS = ((0, P), (P, HALF), (HALF, S))


def tile_picked_haarinp_none_p_kernel(tc, x_words, x_scales, w1, w2, offs, la, lb, out):
    nc = tc.nc
    with ExitStack() as ctx:
        lists = ctx.enter_context(tc.tile_pool(name="lists", bufs=1))
        keep = ctx.enter_context(tc.tile_pool(name="keep", bufs=1))
        psum = ctx.enter_context(tc.psum_pool(name="psum", bufs=1))

        offs_sb = lists.tile([P, S // 16], U16, name="offs_sb")
        la_sb = lists.tile([P, V // 16], U16, name="la_sb")
        lb_sb = lists.tile([P, V // 16], U16, name="lb_sb")

        w1_raw = keep.tile([P, PACK, H], F32, name="w1_raw")
        x_table = keep.tile([P, T], I32, name="x_table", align_bytes=64)
        s_table = keep.tile([P, T], U8, name="s_table", align_bytes=64)
        x_sc = keep.tile([P, S], U8, name="x_sc", align_bytes=64)

        nc.vector.memset(s_table[:].bitcast(I32), 0)
        nc.vector.memset(x_sc[:].bitcast(I32), 0)
        one = keep.tile([P, 1], F32, name="one")
        nc.vector.memset(one[:], 1.0)
        gain = keep.tile([P, 1], F32, name="gain")
        nc.scalar.activation(out=gain[:], in_=one[:], func=COPY, scale=GAIN)

        w1_rows = w1.rearrange("(p j) c -> p j c", j=PACK)
        nc.sync.dma_start(out=w1_raw[:, :2], in_=w1_rows[:, :2])
        nc.sync.dma_start(out=s_table[32:96:4, :].bitcast(I32), in_=x_scales[0].bitcast(I32))
        nc.sync.dma_start(offs_sb[:], offs)
        nc.sync.dma_start(out=w1_raw[:, 2:], in_=w1_rows[:, 2:])
        nc.sync.dma_start(out=x_table[:], in_=x_words[0].rearrange("p n t -> p (n t)").bitcast(I32))
        nc.sync.dma_start(la_sb[:], la)
        nc.sync.dma_start(lb_sb[:], lb)

        s_picked = keep.tile([P, S], U8, name="s_picked", tag="w2_raw", align_bytes=64)
        nc.vector.tensor_copy(out=s_picked[:], in_=s_table[:].indirect(offs_sb[:]))
        for r in range(4):
            nc.sync.dma_start(out=x_sc[r:P:32, :].bitcast(I32), in_=s_picked[32 + 4 * r : 96 : 16, :].bitcast(I32))
        w2_raw = keep.tile([P, PACK, N], F32, name="w2_raw", tag="w2_raw", align_bytes=64)
        nc.sync.dma_start(out=w2_raw[:], in_=w2.rearrange("(p j) c -> p j c", j=PACK))

        w1_grouped = keep.tile([P, PACK * H], BF16, name="w1_grouped", align_bytes=64)
        dst = w1_grouped[:].rearrange("p (h e m j) -> p h m j e", h=2, e=2, j=PACK)
        src = w1_raw[:].rearrange("p j (m h e) -> p h m j e", h=2, e=2)
        nc.vector.tensor_copy(out=dst[:, 0], in_=src[:, 0])
        nc.scalar.copy(out=dst[:, 1], in_=src[:, 1])

        x_codes = keep.tile([P, S], U32, name="x_codes", align_bytes=64)
        w1_codes = [keep.tile([P, P], U32, name="w1_codes%d" % n, align_bytes=64) for n in range(PACK)]
        w1_sc = [keep.tile([P, P], U8, name="w1_sc%d" % n, align_bytes=64) for n in range(PACK)]

        def quantize_w1(n):
            at = SLOT[n] * H
            nc.vector.quantize_mx(out=w1_codes[n][:].bitcast(FP8X4), scales=w1_sc[n][:], in_=w1_grouped[:, at : at + H])

        def pick_words(c0, c1):
            nc.vector.tensor_copy(out=x_codes[:, c0:c1], in_=x_table[:].bitcast(U32).indirect(offs_sb[:, c0 // 16 : c1 // 16]))

        y = [keep.tile([P, S], F32, name="y%d" % n, tag="y%d" % n, align_bytes=64) for n in range(PACK)]

        def first_product(engine, n, c0, c1, bank):
            acc = psum.tile([P, c1 - c0], F32, name="acc", tag="bank%d" % bank)
            nc.tensor.matmul_mx(
                out=acc[:],
                lhsT=w1_codes[n][:].bitcast(FP8X4),
                lhsT_scale=w1_sc[n][:],
                rhs=x_codes[:, c0:c1].bitcast(FP8X4),
                rhs_scale=x_sc[:, c0:c1],
                start=True,
                stop=True,
            )
            if n == 3:
                nc.scalar.activation(out=y[n][:, c0:c1], in_=acc[:], func=COPY, scale=gain[:])
            elif engine == "scalar":
                nc.scalar.copy(out=y[n][:, c0:c1], in_=acc[:])
            else:
                nc.vector.tensor_copy(out=y[n][:, c0:c1], in_=acc[:])

        early = [keep.tile([P, S], F32, name="early%d" % n, tag="early%d" % n, align_bytes=64) for n in range(2)]
        pair = [keep.tile([P, 2 * S], F32, name="pair%d" % n) for n in range(2)]
        window = early + pair
        a = {n: keep.tile([P, V], F32, name="a%d" % n, tag="a%d" % n, align_bytes=64) for n in (0, 1, 3)}
        b = [keep.tile([P, V], F32, name="b%d" % n, tag="b%d" % n, align_bytes=64) for n in range(PACK)]
        df = {0: keep.tile([P, V], F32, name="df0")}

        sm = [None] + [keep.tile([P, V], F32, name="sm%d" % n, tag="sm%d" % n, align_bytes=64) for n in range(1, PACK)]

        def fetch(n):
            nc.scalar.activation(out=b[n][:], in_=y[n][:].indirect(lb_sb[:]), func=COPY)
            if n == 0:
                nc.vector.tensor_copy(out=a[n][:], in_=y[n][:].indirect(la_sb[:]))
            elif n != 2:
                nc.scalar.activation(out=a[n][:], in_=y[n][:].indirect(la_sb[:]), func=COPY)

        def make_sum(n):
            nc.gpsimd.tensor_tensor(sm[n][:], a[n][:], b[n][:], ADD)

        def make_diff(n, tag):
            df[n] = keep.tile([P, V], F32, name="df%d" % n, tag=tag, align_bytes=64)
            nc.gpsimd.tensor_tensor(df[n][:], a[n][:], b[n][:], SUB)

        def put_sum(n):
            nc.vector.tensor_copy(window[n][:].indirect(la_sb[:]), sm[n][:])

        def put_diff(n):
            nc.scalar.activation(out=window[n][:].indirect(lb_sb[:]), in_=df[n][:], func=COPY)

        def join(n):
            if n == 0:
                nc.gpsimd.tensor_scalar(out=pair[n][:, S:], in0=early[n][:], scalar1=1.0, scalar2=0.0, op0=MULT, op1=ADD)
            else:
                nc.vector.tensor_scalar(out=pair[n][:, S:], in0=early[n][:], scalar1=late_gain[:], scalar2=None, op0=MULT)

        src2 = w2_raw[:].rearrange("p j (c i) -> p c j i", i=4)

        def round_z(engine, n, c0, c1):
            src_z = pair[n][:].rearrange("p (h c i) -> p c h i", h=2, i=4)[:, c0 // 4 : c1 // 4]
            at = max(c for c, end in CHUNKS if c <= c0)
            dst_z = z_grouped[at][:, c0 - at : c1 - at, 2 * n : 2 * n + 2].rearrange("p (c i) t -> p c t i", i=4)
            if engine == "scalar":
                nc.scalar.activation(out=dst_z, in_=src_z, func=COPY, scale=last_gain[:])
            elif n == 1:
                nc.vector.tensor_copy(out=dst_z, in_=src_z)
            else:
                nc.vector.tensor_scalar(out=dst_z, in0=src_z, scalar1=last_gain[:], scalar2=None, op0=MULT)

        w2_codes = keep.tile([P, N], U32, name="w2_codes", align_bytes=64)
        w2_sc = {}
        z_codes = keep.tile([P, S], U32, name="z_codes", align_bytes=64)
        z_sc = {0: keep.tile([P, HALF], U8, name="z_sc", align_bytes=64)}

        def quantize_w2(u0, u1, grouped, tag):
            scales = keep.tile([P, (u1 - u0) * P], U8, name="w2_sc", tag=tag, align_bytes=64)
            for u in range(u0, u1):
                w2_sc[u] = scales[:, (u - u0) * P : (u - u0 + 1) * P]
            nc.vector.quantize_mx(out=w2_codes[:, u0 * P : u1 * P].bitcast(FP8X4), scales=scales[:], in_=grouped.rearrange("p c j -> p (c j)"))

        def quantize_z(c0, c1):
            nc.vector.quantize_mx(
                out=z_codes[:, c0:c1].bitcast(FP8X4),
                scales=z_sc[c0 // HALF][:, c0 % HALF : c0 % HALF + c1 - c0],
                in_=z_grouped[c0][:].rearrange("p c t -> p (c t)"),
            )

        done = []

        def second_product(pieces):
            u0, u1 = pieces[0][1], pieces[-1][2]
            s0, s1 = pieces[0][3], pieces[-1][4]
            res = keep.tile([P, u1 - u0, s1 - s0], F32, name="res%d_%d" % (u0, s0))
            for engine, v0, v1, c0, c1 in pieces:
                acc = psum.tile([P, v1 - v0, c1 - c0], F32, name="acc", tag="bank%d" % (len(done) % BANKS))
                done.append(v0)
                for u in range(v0, v1):
                    nc.tensor.matmul_mx(
                        out=acc[:, u - v0, :],
                        lhsT=w2_codes[:, u * P : (u + 1) * P].bitcast(FP8X4),
                        lhsT_scale=w2_sc[u],
                        rhs=z_codes[:, c0:c1].bitcast(FP8X4),
                        rhs_scale=z_sc[c0 // HALF][:, c0 % HALF : c0 % HALF + c1 - c0],
                        start=True,
                        stop=True,
                    )
                if engine == "scalar":
                    nc.scalar.copy(out=res[:, v0 - u0 : v1 - u0, c0 - s0 : c1 - s0], in_=acc[:])
                else:
                    nc.vector.tensor_copy(out=res[:, v0 - u0 : v1 - u0, c0 - s0 : c1 - s0], in_=acc[:])
            nc.sync.dma_start(out=out.rearrange("(u p) c -> p u c", p=P)[:, u0:u1, s0:s1], in_=res[:])

        for n in (0, 2, 1, 3):
            quantize_w1(n)
        pick_words(0, HALF)
        pick_words(HALF, HALF + P)
        pick_words(HALF + P, S)
        first_product("scalar", 0, 0, HALF, 0)
        first_product("vector", 0, HALF, HALF + P, 1)
        first_product("scalar", 0, HALF + P, S, 2)
        first_product("vector", 1, 0, P, 3)
        first_product("scalar", 1, P, HALF, 4)
        fetch(0)
        first_product("vector", 1, HALF, S, 6)
        nc.vector.tensor_tensor(df[0][:], a[0][:], b[0][:], SUB)
        nc.vector.tensor_tensor(window[0][:].indirect(la_sb[:]), a[0][:], b[0][:], ADD)
        first_product("scalar", 3, 0, S, 5)
        fetch(1)
        first_product("vector", 2, 0, S, 6)
        fetch(3)
        put_diff(0)
        fetch(2)
        make_sum(1)
        make_diff(1, "df1")
        put_sum(1)
        a[2] = keep.tile([P, V], F32, name="a2", tag="a1", align_bytes=64)
        nc.vector.tensor_copy(out=a[2][:], in_=y[2][:].indirect(la_sb[:]))
        make_sum(3)
        make_diff(3, "df3")
        join(0)
        make_sum(2)
        make_diff(2, "df2")
        put_sum(3)
        put_sum(2)
        put_diff(1)
        put_diff(3)
        put_diff(2)
        w2_last = keep.tile([P, P, PACK], BF16, name="w2_last", tag="a3", align_bytes=64)
        nc.gpsimd.tensor_scalar(out=w2_last[:], in0=w2_raw[:].rearrange("p j c -> p c j")[:, 3 * P :], scalar1=1.0, scalar2=0.0, op0=MULT, op1=ADD)
        late_gain = keep.tile([P, 1], F32, name="late_gain", tag="b2", align_bytes=64)
        nc.vector.memset(late_gain[:], GAIN)
        w2_first = keep.tile([P, 3 * P, PACK], BF16, name="w2_first", tag="a1", align_bytes=64)
        nc.vector.tensor_copy(out=w2_first[:].rearrange("p (c i) j -> p c j i", i=4), in_=src2[:, : 3 * P // 4])
        join(1)

        z_grouped = {
            c0: keep.tile([P, c1 - c0, PACK], BF16, name="z_grouped%d" % c0, tag=tag, align_bytes=64)
            for (c0, c1), tag in zip(CHUNKS, ("z_first", "z_second", "z_third"))
        }
        quantize_w2(0, 3, w2_first[:], "w2_sc0")
        last_gain = keep.tile([P, 1], F32, name="last_gain", tag="early1", align_bytes=64)
        nc.vector.memset(last_gain[:], GAIN)
        for c0, c1 in CHUNKS:
            round_z("vector", 1, c0, c1)
        round_z("vector", 0, 0, P)
        round_z("vector", 0, P, HALF)
        round_z("scalar", 0, HALF, S)
        quantize_z(0, P)
        quantize_z(P, HALF)
        quantize_w2(3, 4, w2_last[:], "z_first")
        z_sc[1] = keep.tile([P, HALF], U8, name="z_sc", tag="z_second", align_bytes=64)
        quantize_z(HALF, S)
        second_product([("scalar", 0, 1, 0, P)])
        second_product([("scalar", 1, 2, 0, P)])
        second_product([("scalar", 0, 2, P, HALF)])
        second_product([("vector", 2, 3, 0, HALF)])
        second_product([("scalar", 3, 4, 0, HALF)])
        second_product([("vector", 0, 1, HALF, S)])
        second_product([("scalar", 1, 2, HALF, S)])
        second_product([("vector", 2, 3, HALF, S)])
        second_product([("scalar", 3, 4, HALF, 3 * P)])
        second_product([("vector", 3, 4, 3 * P, S)])
